import numpy as np
import ml_dtypes


def mxq(x, axis, fmt="e4m3"):
    dtype, down = {"e4m3": (ml_dtypes.float8_e4m3fn, 7), "e5m2": (ml_dtypes.float8_e5m2, 14)}[fmt]
    v = np.moveaxis(np.asarray(x, np.float32).astype(ml_dtypes.bfloat16).astype(np.float64), axis, -1)
    blocks = v.reshape(v.shape[:-1] + (-1, 32))
    amax = np.abs(blocks).max(-1, keepdims=True)
    byte = np.maximum(np.where(amax > 0, np.frexp(amax)[1] - 1 + 127, 0) - down, 1)
    scale = np.exp2(byte - 127.0)
    codes = (blocks / scale).astype(np.float32).astype(dtype).astype(np.float64)
    return np.moveaxis((codes * scale).reshape(v.shape), -1, axis)


WIDE = False


def mx_kscale(k):
    if not WIDE:
        return np.ones(k)
    levels = np.array([10, -10, 5, -5, 0])
    if k % 512:
        return np.exp2(np.random.permutation(np.resize(levels, k // 32))).repeat(32)
    a = np.empty((k // 512, 16))
    for p in range(k // 512):
        a[p, :8] = np.random.permutation(np.resize(levels, 8))
        for g in range(8):
            far = levels[np.abs(levels - a[p, g]) >= 10]
            a[p, g + 8] = far[np.random.randint(len(far))]
    return np.exp2(a.ravel()).repeat(32)


def f64(x):
    return np.asarray(x).astype(np.float64)


def striped(idx):
    return np.tile(idx.reshape(-1, 16).T, (8, 1)).astype(np.uint16)


def unstriped(offs):
    return offs[:16].T.reshape(-1).astype(np.int64)


def striped8(idx):
    return np.concatenate([v.reshape(-1, 16).T for v in idx]).astype(np.uint16)


def unstriped8(offs):
    return np.stack([offs[16 * g:16 * g + 16].T.reshape(-1) for g in range(8)]).astype(np.int64)


E2M1 = np.array([0.0, 0.5, 1.0, 1.5, 2.0, 3.0, 4.0, 6.0, -0.0, -0.5, -1.0, -1.5, -2.0, -3.0, -4.0, -6.0])


def pack_weight(w, fmt):
    k, n = w.shape
    w = f64(np.asarray(w, np.float32).astype(ml_dtypes.bfloat16)).reshape(k // 32, 32, n)
    amax = np.abs(w).max(1)
    if fmt == "e4m3":
        byte = np.frexp(amax)[1] - 1 + 127 - 7
    else:
        mant, ex = np.frexp(amax / 6.0)
        byte = np.where(mant > 0.5, ex, ex - 1) + 127
    byte = np.clip(np.where(amax > 0, byte, 1), 1, 254)
    scaled = (w * np.exp2(127.0 - byte)[:, None, :]).reshape(k, n).astype(np.float32)
    by_word = np.ascontiguousarray(scaled.reshape(k // 512, 128, 4, n).transpose(0, 1, 3, 2))
    if fmt == "e4m3":
        words = by_word.astype(ml_dtypes.float8_e4m3fn).view(np.uint8)
    else:
        c = by_word.astype(ml_dtypes.float4_e2m1fn).view(np.uint8) & 0xF
        words = (c[..., 0::2] | (c[..., 1::2] << 4)).reshape(k // 512, 128, 2 * n)
    return np.ascontiguousarray(words), np.ascontiguousarray(byte.astype(np.uint8).reshape(k // 512, 16, n))


def unpack_weight(words, scales, fmt):
    g, _, n = scales.shape
    words = np.ascontiguousarray(words).reshape(g, 128, n, -1)
    if fmt == "e4m3":
        vals = words.view(ml_dtypes.float8_e4m3fn).astype(np.float64)
    else:
        nib = np.empty((g, 128, n, 4), np.uint8)
        nib[..., 0::2] = words & 0xF
        nib[..., 1::2] = words >> 4
        vals = E2M1[nib]
    vals = vals * np.repeat(np.exp2(scales.astype(np.float64) - 127.0), 8, axis=1)[..., None]
    return vals.transpose(0, 1, 3, 2).reshape(g * 512, n)


def pack_table(v):
    words, scales = pack_weight(v, "e4m3")
    return np.concatenate([words.reshape(words.shape[0], -1), scales.reshape(scales.shape[0], -1)], axis=1)


def unpack_table(tab):
    g, t = tab.shape[0], tab.shape[1] // 528
    return unpack_weight(tab[:, :512 * t].reshape(g, 128, t, 4), tab[:, 512 * t:].reshape(g, 16, t), "e4m3")


def gelu(v):
    return 0.5 * v * (1.0 + np.tanh(np.sqrt(2.0 / np.pi) * (v + 0.044715 * v**3)))


K, M, T, S = 512, 256, 4096, 2048


def setup_inputs():
    n = np.random.standard_normal
    s = mx_kscale(K)[:, None]
    return {
        "tab": pack_table(n((K, T)) * s),
        "w": (n((K, M)) / np.sqrt(K) / s).astype(np.float32),
        "b": (0.3 * n(256)).astype(np.float32),
        "wgo": np.repeat(np.random.uniform(0.5, 2.0, (8, S)), 16, axis=0).astype(np.float32),
        "offs": striped(np.random.permutation(T)[:S]),
        "offs2": striped8(np.stack([np.random.permutation(T)[:S] for _ in range(8)])),
    }


def reference(tab, w, b, wgo, offs, offs2):
    tab_ = unpack_table(tab)[:, unstriped(offs)]
    w_ = mxq(f64(w), 0, "e4m3")
    y = w_.T @ tab_
    place = unstriped8(offs2)[np.arange(M) % 128 // 16]
    out = np.zeros((M, T))
    out[np.arange(M)[:, None], place] = f64(wgo)[np.arange(M) % 128] * (gelu(y + f64(b)[:, None]))
    return out

@@ -1,0 +1,112 @@
+import concourse.mybir as mybir
+
+K, M, T, S = 512, 256, 4096, 2048
+P = 128
+FLOPS = 2 * K * M * S
+
+F32 = mybir.dt.float32
+BF16 = mybir.dt.bfloat16
+I32 = mybir.dt.int32
+U32 = mybir.dt.uint32
+U16 = mybir.dt.uint16
+U8 = mybir.dt.uint8
+FP8X4 = mybir.dt.float8_e4m3fn_x4
+COPY = mybir.ActivationFunctionType.Copy
+GELU = mybir.ActivationFunctionType.Gelu_apprx_tanh
+MULT = mybir.AluOpType.mult
+
+GATHER = 1024
+SCATTER = 1024
+BANK = 512
+CLEAR = 1024
+
+
+def tile_list_tabhs_gelu_kernel(tc, tab, w, b, wgo, offs, offs2, out):
+    nc = tc.nc
+    with (
+        tc.tile_pool(name="keep", bufs=1) as keep,
+        tc.psum_pool(name="psum", bufs=1) as psum,
+    ):
+        idx = keep.tile([P, S // 16], U16, name="idx")
+        idx2 = keep.tile([P, S // 16], U16, name="idx2")
+        zero = keep.tile([P, 1], F32, tag="small", name="zero")
+        warm = keep.tile([P, 1], F32, tag="load", name="warm")
+        plane = keep.tile([P, T], U8, tag="mid", name="plane", align_bytes=64)
+        words = keep.tile([P, T], I32, tag="wide", name="words", align_bytes=64)
+        window0 = keep.tile([P, T], F32, name="window0")
+
+        nc.gpsimd.memset(zero[:], 0.0)
+        nc.gpsimd.memset(plane[:].bitcast(I32), 0)
+        nc.gpsimd.memset(words[:, 0:8], 0)
+        nc.sync.dma_start(idx[:], offs)
+        nc.sync.dma_start(idx2[:], offs2)
+        nc.scalar.activation(warm[:], zero[:], GELU)
+        scale_rows = tab[0, 512 * T : 528 * T].rearrange("(q t) -> q t", t=T)
+        for quad in range(4):
+            nc.sync.dma_start(
+                plane[32 * quad : 32 * quad + 4, :].bitcast(I32),
+                scale_rows[4 * quad : 4 * quad + 4, :].bitcast(I32),
+            )
+        nc.sync.dma_start(words[:], tab[0, 0 : 512 * T].rearrange("(p c) -> p c", p=P).bitcast(I32))
+        w_raw = keep.tile([P, 4, M], F32, tag="load", name="w_raw")
+        nc.sync.dma_start(w_raw[:], w.rearrange("(p j) n -> p j n", j=4))
+        bias = keep.tile([P, 2], F32, tag="small", name="bias")
+        with nc.allow_non_contiguous_dma(reason="256 values, one to a partition"):
+            nc.sync.dma_start(bias[:], b.rearrange("(c p) -> p c", p=P))
+        nc.vector.memset(window0[:, 0 : T // 2], 0.0)
+        for c in range(T // 2, T, CLEAR):
+            nc.gpsimd.memset(window0[:, c : c + CLEAR], 0.0)
+
+        w_group = keep.tile([P, M, 4], BF16, tag="late", name="w_group", align_bytes=64)
+        w_codes = keep.tile([P, M], U32, name="w_codes", align_bytes=64)
+        w_scales = keep.tile([P, M], U8, name="w_scales", align_bytes=64)
+        nc.scalar.activation(w_group[:], w_raw[:].rearrange("p j n -> p n j"), COPY)
+
+        g_scales = keep.tile([P, S], U8, name="g_scales", align_bytes=64)
+        nc.vector.tensor_copy(g_scales[:], plane[:].indirect(idx[:]))
+        factor = keep.tile([P, S], F32, tag="mid", name="factor", align_bytes=64)
+        for s in range(0, S, SCATTER):
+            nc.sync.dma_start(factor[:, s : s + SCATTER], wgo[:, s : s + SCATTER])
+
+        def gather_words(codes, s):
+            nc.vector.tensor_copy(
+                codes[:],
+                words[:].bitcast(U32).indirect(idx[:, s // 16 : (s + GATHER) // 16]),
+            )
+
+        codes0 = keep.tile([P, GATHER], U32, name="codes0", align_bytes=64)
+        gather_words(codes0, 0)
+        nc.vector.quantize_mx(
+            out=w_codes[:].bitcast(FP8X4),
+            scales=w_scales[:],
+            in_=w_group[:].rearrange("p n j -> p (n j)"),
+        )
+        codes1 = keep.tile([P, GATHER], U32, tag="late", name="codes1", align_bytes=64)
+        gather_words(codes1, GATHER)
+        codes = [codes0, codes1]
+
+        window1 = keep.tile([P, T], F32, tag="wide", name="window1", align_bytes=64)
+        nc.gpsimd.memset(window1[:], 0.0)
+        windows = [window0, window1]
+        y = keep.tile([P, 2, S], F32, name="y")
+        for m in range(2):
+            for s in range(0, S, BANK):
+                bank = psum.tile([P, BANK], F32, name="bank%d_%d" % (m, s // BANK))
+                nc.tensor.matmul_mx(
+                    out=bank[:],
+                    lhsT=w_codes[:, P * m : P * m + P].bitcast(FP8X4),
+                    lhsT_scale=w_scales[:, P * m : P * m + P],
+                    rhs=codes[s // GATHER][:, s % GATHER : s % GATHER + BANK].bitcast(FP8X4),
+                    rhs_scale=g_scales[:, s : s + BANK],
+                    start=True,
+                    stop=True,
+                )
+                nc.scalar.activation(y[:, m, s : s + BANK], bank[:], GELU, bias=bias[:, m : m + 1])
+            for s in range(0, S, SCATTER):
+                nc.vector.tensor_tensor(
+                    windows[m][:].indirect(idx2[:, s // 16 : (s + SCATTER) // 16]),
+                    y[:, m, s : s + SCATTER],
+                    factor[:, s : s + SCATTER],
+                    MULT,
+                )
+            nc.sync.dma_start(out[P * m : P * m + P, :], windows[m][:])

@@ -15,10 +15,8 @@ COPY = mybir.ActivationFunctionType.Copy
 GELU = mybir.ActivationFunctionType.Gelu_apprx_tanh
 MULT = mybir.AluOpType.mult
 
-GATHER = 1024
-SCATTER = 1024
+HALF = 1024
 BANK = 512
-CLEAR = 1024
 
 
 def tile_list_tabhs_gelu_kernel(tc, tab, w, b, wgo, offs, offs2, out):
@@ -29,64 +27,69 @@ def tile_list_tabhs_gelu_kernel(tc, tab, w, b, wgo, offs, offs2, out):
     ):
         idx = keep.tile([P, S // 16], U16, name="idx")
         idx2 = keep.tile([P, S // 16], U16, name="idx2")
-        zero = keep.tile([P, 1], F32, tag="small", name="zero")
+        rows = keep.tile([P, T], U8, name="rows", align_bytes=64)
+        seed = keep.tile([P, 1], F32, tag="wide", name="seed", align_bytes=64)
+        zero = keep.tile([P, 1], F32, tag="first", name="zero", align_bytes=64)
         warm = keep.tile([P, 1], F32, tag="load", name="warm")
-        plane = keep.tile([P, T], U8, tag="mid", name="plane", align_bytes=64)
-        words = keep.tile([P, T], I32, tag="wide", name="words", align_bytes=64)
-        window0 = keep.tile([P, T], F32, name="window0")
+        planes = [keep.tile([P, HALF], U8, name="plane%d" % h, align_bytes=64) for h in range(2)]
 
-        nc.gpsimd.memset(zero[:], 0.0)
-        nc.gpsimd.memset(plane[:].bitcast(I32), 0)
-        nc.gpsimd.memset(words[:, 0:8], 0)
+        nc.vector.memset(rows[:].bitcast(I32), 0)
+        nc.vector.memset(seed[:], 0.0)
+        nc.vector.tensor_copy(zero[:], seed[:])
+        for h in range(2):
+            nc.vector.memset(planes[h][:].bitcast(I32), 0)
         nc.sync.dma_start(idx[:], offs)
-        nc.sync.dma_start(idx2[:], offs2)
-        nc.scalar.activation(warm[:], zero[:], GELU)
         scale_rows = tab[0, 512 * T : 528 * T].rearrange("(q t) -> q t", t=T)
-        for quad in range(4):
-            nc.sync.dma_start(
-                plane[32 * quad : 32 * quad + 4, :].bitcast(I32),
-                scale_rows[4 * quad : 4 * quad + 4, :].bitcast(I32),
-            )
+        nc.sync.dma_start(rows[0:P:8, :].bitcast(I32), scale_rows.bitcast(I32))
+        nc.scalar.activation(warm[:], zero[:], GELU)
+        words = keep.tile([P, T], I32, tag="wide", name="words", align_bytes=64)
         nc.sync.dma_start(words[:], tab[0, 0 : 512 * T].rearrange("(p c) -> p c", p=P).bitcast(I32))
-        w_raw = keep.tile([P, 4, M], F32, tag="load", name="w_raw")
-        nc.sync.dma_start(w_raw[:], w.rearrange("(p j) n -> p j n", j=4))
-        bias = keep.tile([P, 2], F32, tag="small", name="bias")
+        params = keep.tile([P, 4 * M + 8], F32, tag="load", name="params")
+        w_raw = params[:, 0 : 4 * M].rearrange("p (j n) -> p j n", j=4)
+        bias = params[:, 4 * M : 4 * M + 2]
+        nc.sync.dma_start(w_raw, w.rearrange("(p j) n -> p j n", j=4))
         with nc.allow_non_contiguous_dma(reason="256 values, one to a partition"):
-            nc.sync.dma_start(bias[:], b.rearrange("(c p) -> p c", p=P))
-        nc.vector.memset(window0[:, 0 : T // 2], 0.0)
-        for c in range(T // 2, T, CLEAR):
-            nc.gpsimd.memset(window0[:, c : c + CLEAR], 0.0)
+            nc.sync.dma_start(bias, b.rearrange("(c p) -> p c", p=P))
+        nc.sync.dma_start(idx2[:], offs2)
+
+        window0 = keep.tile([P, T], F32, tag="first", name="window0", align_bytes=64)
+        nc.gpsimd.memset(window0[:], 0.0)
+
+        for h in range(2):
+            picked = keep.tile([P, HALF], U8, tag="picked%d" % h, name="picked%d" % h, align_bytes=64)
+            nc.vector.tensor_copy(picked[:], rows[:].indirect(idx[:, h * HALF // 16 : (h + 1) * HALF // 16]))
+            for r in range(4):
+                nc.scalar.dma_start(planes[h][r:P:32, :].bitcast(I32), picked[8 * r : P : 32, :].bitcast(I32))
+
+        factor0 = keep.tile([P, HALF], F32, tag="picked0", name="factor0", align_bytes=64)
+        nc.sync.dma_start(factor0[:], wgo[:, 0:HALF])
 
         w_group = keep.tile([P, M, 4], BF16, tag="late", name="w_group", align_bytes=64)
         w_codes = keep.tile([P, M], U32, name="w_codes", align_bytes=64)
         w_scales = keep.tile([P, M], U8, name="w_scales", align_bytes=64)
-        nc.scalar.activation(w_group[:], w_raw[:].rearrange("p j n -> p n j"), COPY)
+        nc.scalar.activation(w_group[:], w_raw.rearrange("p j n -> p n j"), COPY)
 
-        g_scales = keep.tile([P, S], U8, name="g_scales", align_bytes=64)
-        nc.vector.tensor_copy(g_scales[:], plane[:].indirect(idx[:]))
-        factor = keep.tile([P, S], F32, tag="mid", name="factor", align_bytes=64)
-        for s in range(0, S, SCATTER):
-            nc.sync.dma_start(factor[:, s : s + SCATTER], wgo[:, s : s + SCATTER])
-
-        def gather_words(codes, s):
+        def gather_words(h):
+            codes = keep.tile([P, HALF], U32, tag=("early", "late")[h], name="codes%d" % h, align_bytes=64)
             nc.vector.tensor_copy(
                 codes[:],
-                words[:].bitcast(U32).indirect(idx[:, s // 16 : (s + GATHER) // 16]),
+                words[:].bitcast(U32).indirect(idx[:, h * HALF // 16 : (h + 1) * HALF // 16]),
             )
+            return codes
 
-        codes0 = keep.tile([P, GATHER], U32, name="codes0", align_bytes=64)
-        gather_words(codes0, 0)
+        codes0 = gather_words(0)
         nc.vector.quantize_mx(
             out=w_codes[:].bitcast(FP8X4),
             scales=w_scales[:],
             in_=w_group[:].rearrange("p n j -> p (n j)"),
         )
-        codes1 = keep.tile([P, GATHER], U32, tag="late", name="codes1", align_bytes=64)
-        gather_words(codes1, GATHER)
-        codes = [codes0, codes1]
+        codes = [codes0, gather_words(1)]
 
-        window1 = keep.tile([P, T], F32, tag="wide", name="window1", align_bytes=64)
+        window1 = keep.tile([P, T], F32, tag="late", name="window1", align_bytes=64)
         nc.gpsimd.memset(window1[:], 0.0)
+        factor1 = keep.tile([P, HALF], F32, tag="wide", name="factor1", align_bytes=64)
+        nc.sync.dma_start(factor1[:], wgo[:, HALF:S])
+        factors = [factor0, factor1]
         windows = [window0, window1]
         y = keep.tile([P, 2, S], F32, name="y")
         for m in range(2):
@@ -96,17 +99,17 @@ def tile_list_tabhs_gelu_kernel(tc, tab, w, b, wgo, offs, offs2, out):
                     out=bank[:],
                     lhsT=w_codes[:, P * m : P * m + P].bitcast(FP8X4),
                     lhsT_scale=w_scales[:, P * m : P * m + P],
-                    rhs=codes[s // GATHER][:, s % GATHER : s % GATHER + BANK].bitcast(FP8X4),
-                    rhs_scale=g_scales[:, s : s + BANK],
+                    rhs=codes[s // HALF][:, s % HALF : s % HALF + BANK].bitcast(FP8X4),
+                    rhs_scale=planes[s // HALF][:, s % HALF : s % HALF + BANK],
                     start=True,
                     stop=True,
                 )
                 nc.scalar.activation(y[:, m, s : s + BANK], bank[:], GELU, bias=bias[:, m : m + 1])
-            for s in range(0, S, SCATTER):
+            for h in range(2):
                 nc.vector.tensor_tensor(
-                    windows[m][:].indirect(idx2[:, s // 16 : (s + SCATTER) // 16]),
-                    y[:, m, s : s + SCATTER],
-                    factor[:, s : s + SCATTER],
+                    windows[m][:].indirect(idx2[:, h * HALF // 16 : (h + 1) * HALF // 16]),
+                    y[:, m, h * HALF : (h + 1) * HALF],
+                    factors[h][:],
                     MULT,
                 )
             nc.sync.dma_start(out[P * m : P * m + P, :], windows[m][:])

@@ -38,6 +38,8 @@ def tile_list_tabhs_gelu_kernel(tc, tab, w, b, wgo, offs, offs2, out):
         nc.vector.tensor_copy(zero[:], seed[:])
         for h in range(2):
             nc.vector.memset(planes[h][:].bitcast(I32), 0)
+        window1 = keep.tile([P, T], F32, name="window1", align_bytes=64)
+        nc.vector.memset(window1[:], 0.0)
         nc.sync.dma_start(idx[:], offs)
         scale_rows = tab[0, 512 * T : 528 * T].rearrange("(q t) -> q t", t=T)
         nc.sync.dma_start(rows[0:P:8, :].bitcast(I32), scale_rows.bitcast(I32))
@@ -69,47 +71,47 @@ def tile_list_tabhs_gelu_kernel(tc, tab, w, b, wgo, offs, offs2, out):
         w_scales = keep.tile([P, M], U8, name="w_scales", align_bytes=64)
         nc.scalar.activation(w_group[:], w_raw.rearrange("p j n -> p n j"), COPY)
 
-        def gather_words(h):
-            codes = keep.tile([P, HALF], U32, tag=("early", "late")[h], name="codes%d" % h, align_bytes=64)
+        def gather_words(codes, h):
             nc.vector.tensor_copy(
                 codes[:],
                 words[:].bitcast(U32).indirect(idx[:, h * HALF // 16 : (h + 1) * HALF // 16]),
             )
-            return codes
 
-        codes0 = gather_words(0)
+        codes0 = keep.tile([P, HALF], U32, name="codes0", align_bytes=64)
+        gather_words(codes0, 0)
         nc.vector.quantize_mx(
             out=w_codes[:].bitcast(FP8X4),
             scales=w_scales[:],
             in_=w_group[:].rearrange("p n j -> p (n j)"),
         )
-        codes = [codes0, gather_words(1)]
+        codes1 = keep.tile([P, HALF], U32, tag="late", name="codes1", align_bytes=64)
+        gather_words(codes1, 1)
+        codes = [codes0, codes1]
 
-        window1 = keep.tile([P, T], F32, tag="late", name="window1", align_bytes=64)
-        nc.gpsimd.memset(window1[:], 0.0)
         factor1 = keep.tile([P, HALF], F32, tag="wide", name="factor1", align_bytes=64)
         nc.sync.dma_start(factor1[:], wgo[:, HALF:S])
         factors = [factor0, factor1]
         windows = [window0, window1]
-        y = keep.tile([P, 2, S], F32, name="y")
-        for m in range(2):
-            for s in range(0, S, BANK):
-                bank = psum.tile([P, BANK], F32, name="bank%d_%d" % (m, s // BANK))
-                nc.tensor.matmul_mx(
-                    out=bank[:],
-                    lhsT=w_codes[:, P * m : P * m + P].bitcast(FP8X4),
-                    lhsT_scale=w_scales[:, P * m : P * m + P],
-                    rhs=codes[s // HALF][:, s % HALF : s % HALF + BANK].bitcast(FP8X4),
-                    rhs_scale=planes[s // HALF][:, s % HALF : s % HALF + BANK],
-                    start=True,
-                    stop=True,
-                )
-                nc.scalar.activation(y[:, m, s : s + BANK], bank[:], GELU, bias=bias[:, m : m + 1])
-            for h in range(2):
+        y = keep.tile([P, 4, HALF], F32, name="y")
+        for h in range(2):
+            for m in range(2):
+                for s in range(0, HALF, BANK):
+                    bank = psum.tile([P, BANK], F32, name="bank%d_%d_%d" % (h, m, s // BANK))
+                    nc.tensor.matmul_mx(
+                        out=bank[:],
+                        lhsT=w_codes[:, P * m : P * m + P].bitcast(FP8X4),
+                        lhsT_scale=w_scales[:, P * m : P * m + P],
+                        rhs=codes[h][:, s : s + BANK].bitcast(FP8X4),
+                        rhs_scale=planes[h][:, s : s + BANK],
+                        start=True,
+                        stop=True,
+                    )
+                    nc.scalar.activation(y[:, 2 * h + m, s : s + BANK], bank[:], GELU, bias=bias[:, m : m + 1])
                 nc.vector.tensor_tensor(
                     windows[m][:].indirect(idx2[:, h * HALF // 16 : (h + 1) * HALF // 16]),
-                    y[:, m, h * HALF : (h + 1) * HALF],
+                    y[:, 2 * h + m, :],
                     factors[h][:],
                     MULT,
                 )
+        for m in range(2):
             nc.sync.dma_start(out[P * m : P * m + P, :], windows[m][:])

@@ -61,10 +61,10 @@ def tile_list_tabhs_gelu_kernel(tc, tab, w, b, wgo, offs, offs2, out):
             picked = keep.tile([P, HALF], U8, tag="picked%d" % h, name="picked%d" % h, align_bytes=64)
             nc.vector.tensor_copy(picked[:], rows[:].indirect(idx[:, h * HALF // 16 : (h + 1) * HALF // 16]))
             for r in range(4):
-                nc.scalar.dma_start(planes[h][r:P:32, :].bitcast(I32), picked[8 * r : P : 32, :].bitcast(I32))
+                nc.sync.dma_start(planes[h][r:P:32, :].bitcast(I32), picked[8 * r : P : 32, :].bitcast(I32))
 
-        factor0 = keep.tile([P, HALF], F32, tag="picked0", name="factor0", align_bytes=64)
-        nc.sync.dma_start(factor0[:], wgo[:, 0:HALF])
+        factor0 = keep.tile([P, BANK], F32, tag="picked0", name="factor0", align_bytes=64)
+        nc.sync.dma_start(factor0[:], wgo[:, 0:BANK])
 
         w_group = keep.tile([P, M, 4], BF16, tag="late", name="w_group", align_bytes=64)
         w_codes = keep.tile([P, M], U32, name="w_codes", align_bytes=64)
@@ -88,29 +88,29 @@ def tile_list_tabhs_gelu_kernel(tc, tab, w, b, wgo, offs, offs2, out):
         gather_words(codes1, 1)
         codes = [codes0, codes1]
 
-        factor1 = keep.tile([P, HALF], F32, tag="wide", name="factor1", align_bytes=64)
-        nc.sync.dma_start(factor1[:], wgo[:, HALF:S])
+        factor1 = keep.tile([P, S - BANK], F32, tag="wide", name="factor1", align_bytes=64)
+        nc.sync.dma_start(factor1[:], wgo[:, BANK:S])
         factors = [factor0, factor1]
         windows = [window0, window1]
-        y = keep.tile([P, 4, HALF], F32, name="y")
-        for h in range(2):
+        y = [keep.tile([P, S], F32, name="y%d" % m) for m in range(2)]
+        for (lo, hi), factor in zip(((0, BANK), (BANK, S)), factors):
             for m in range(2):
-                for s in range(0, HALF, BANK):
-                    bank = psum.tile([P, BANK], F32, name="bank%d_%d_%d" % (h, m, s // BANK))
+                for s in range(lo, hi, BANK):
+                    bank = psum.tile([P, BANK], F32, name="bank%d_%d" % (m, s // BANK))
                     nc.tensor.matmul_mx(
                         out=bank[:],
                         lhsT=w_codes[:, P * m : P * m + P].bitcast(FP8X4),
                         lhsT_scale=w_scales[:, P * m : P * m + P],
-                        rhs=codes[h][:, s : s + BANK].bitcast(FP8X4),
-                        rhs_scale=planes[h][:, s : s + BANK],
+                        rhs=codes[s // HALF][:, s % HALF : s % HALF + BANK].bitcast(FP8X4),
+                        rhs_scale=planes[s // HALF][:, s % HALF : s % HALF + BANK],
                         start=True,
                         stop=True,
                     )
-                    nc.scalar.activation(y[:, 2 * h + m, s : s + BANK], bank[:], GELU, bias=bias[:, m : m + 1])
+                    nc.scalar.activation(y[m][:, s : s + BANK], bank[:], GELU, bias=bias[:, m : m + 1])
                 nc.vector.tensor_tensor(
-                    windows[m][:].indirect(idx2[:, h * HALF // 16 : (h + 1) * HALF // 16]),
-                    y[:, 2 * h + m, :],
-                    factors[h][:],
+                    windows[m][:].indirect(idx2[:, lo // 16 : hi // 16]),
+                    y[m][:, lo:hi],
+                    factor[:],
                     MULT,
                 )
         for m in range(2):

@@ -23,21 +23,20 @@ def tile_list_tabhs_gelu_kernel(tc, tab, w, b, wgo, offs, offs2, out):
     nc = tc.nc
     with (
         tc.tile_pool(name="keep", bufs=1) as keep,
+        tc.tile_pool(name="load", bufs=1) as load,
         tc.psum_pool(name="psum", bufs=1) as psum,
     ):
         idx = keep.tile([P, S // 16], U16, name="idx")
         idx2 = keep.tile([P, S // 16], U16, name="idx2")
         rows = keep.tile([P, T], U8, name="rows", align_bytes=64)
-        seed = keep.tile([P, 1], F32, tag="wide", name="seed", align_bytes=64)
-        zero = keep.tile([P, 1], F32, tag="first", name="zero", align_bytes=64)
-        warm = keep.tile([P, 1], F32, tag="load", name="warm")
+        seed = keep.tile([P, 32], F32, tag="wide", name="seed", align_bytes=64)
+        zero = keep.tile([P, 32], F32, tag="first", name="zero", align_bytes=64)
+        warm = load.tile([P, 32], F32, name="warm", align_bytes=64, offset=16 * M - 64)
         planes = [keep.tile([P, HALF], U8, name="plane%d" % h, align_bytes=64) for h in range(2)]
 
-        nc.vector.memset(rows[:].bitcast(I32), 0)
         nc.vector.memset(seed[:], 0.0)
+        nc.vector.memset(rows[:].bitcast(I32), 0)
         nc.vector.tensor_copy(zero[:], seed[:])
-        for h in range(2):
-            nc.vector.memset(planes[h][:].bitcast(I32), 0)
         window1 = keep.tile([P, T], F32, name="window1", align_bytes=64)
         nc.vector.memset(window1[:], 0.0)
         nc.sync.dma_start(idx[:], offs)
@@ -46,12 +45,11 @@ def tile_list_tabhs_gelu_kernel(tc, tab, w, b, wgo, offs, offs2, out):
         nc.scalar.activation(warm[:], zero[:], GELU)
         words = keep.tile([P, T], I32, tag="wide", name="words", align_bytes=64)
         nc.sync.dma_start(words[:], tab[0, 0 : 512 * T].rearrange("(p c) -> p c", p=P).bitcast(I32))
-        params = keep.tile([P, 4 * M + 8], F32, tag="load", name="params")
-        w_raw = params[:, 0 : 4 * M].rearrange("p (j n) -> p j n", j=4)
-        bias = params[:, 4 * M : 4 * M + 2]
-        nc.sync.dma_start(w_raw, w.rearrange("(p j) n -> p j n", j=4))
+        w_raw = load.tile([P, 4, M], F32, name="w_raw", align_bytes=64, offset=0)
+        bias = load.tile([P, 2], F32, name="bias", align_bytes=64, offset=16 * M)
+        nc.sync.dma_start(w_raw[:], w.rearrange("(p j) n -> p j n", j=4))
         with nc.allow_non_contiguous_dma(reason="256 values, one to a partition"):
-            nc.sync.dma_start(bias, b.rearrange("(c p) -> p c", p=P))
+            nc.sync.dma_start(bias[:], b.rearrange("(c p) -> p c", p=P))
         nc.sync.dma_start(idx2[:], offs2)
 
         window0 = keep.tile([P, T], F32, tag="first", name="window0", align_bytes=64)
@@ -66,10 +64,20 @@ def tile_list_tabhs_gelu_kernel(tc, tab, w, b, wgo, offs, offs2, out):
         factor0 = keep.tile([P, BANK], F32, tag="picked0", name="factor0", align_bytes=64)
         nc.sync.dma_start(factor0[:], wgo[:, 0:BANK])
 
-        w_group = keep.tile([P, M, 4], BF16, tag="late", name="w_group", align_bytes=64)
-        w_codes = keep.tile([P, M], U32, name="w_codes", align_bytes=64)
-        w_scales = keep.tile([P, M], U8, name="w_scales", align_bytes=64)
-        nc.scalar.activation(w_group[:], w_raw.rearrange("p j n -> p n j"), COPY)
+        groups = [
+            keep.tile([P, P, 4], BF16, tag="late", name="group0", align_bytes=64),
+            keep.tile([P, P, 4], BF16, name="group1", align_bytes=64),
+        ]
+        for m in range(2):
+            nc.scalar.activation(groups[m][:], w_raw[:, :, P * m : P * m + P].rearrange("p j n -> p n j"), COPY)
+        w_scales = [keep.tile([P, P], U8, name="w_scales%d" % m, align_bytes=64) for m in range(2)]
+
+        def quantize(w_codes, m):
+            nc.vector.quantize_mx(
+                out=w_codes[:].bitcast(FP8X4),
+                scales=w_scales[m][:],
+                in_=groups[m][:].rearrange("p n j -> p (n j)"),
+            )
 
         def gather_words(codes, h):
             nc.vector.tensor_copy(
@@ -79,14 +87,14 @@ def tile_list_tabhs_gelu_kernel(tc, tab, w, b, wgo, offs, offs2, out):
 
         codes0 = keep.tile([P, HALF], U32, name="codes0", align_bytes=64)
         gather_words(codes0, 0)
-        nc.vector.quantize_mx(
-            out=w_codes[:].bitcast(FP8X4),
-            scales=w_scales[:],
-            in_=w_group[:].rearrange("p n j -> p (n j)"),
-        )
-        codes1 = keep.tile([P, HALF], U32, tag="late", name="codes1", align_bytes=64)
+        w_codes0 = keep.tile([P, P], U32, name="w_codes0", align_bytes=64)
+        quantize(w_codes0, 0)
+        codes1 = load.tile([P, HALF], U32, name="codes1", align_bytes=64, offset=0)
         gather_words(codes1, 1)
         codes = [codes0, codes1]
+        w_codes1 = keep.tile([P, P], U32, tag="late", name="w_codes1", align_bytes=64)
+        quantize(w_codes1, 1)
+        w_codes = [w_codes0, w_codes1]
 
         factor1 = keep.tile([P, S - BANK], F32, tag="wide", name="factor1", align_bytes=64)
         nc.sync.dma_start(factor1[:], wgo[:, BANK:S])
@@ -99,8 +107,8 @@ def tile_list_tabhs_gelu_kernel(tc, tab, w, b, wgo, offs, offs2, out):
                     bank = psum.tile([P, BANK], F32, name="bank%d_%d" % (m, s // BANK))
                     nc.tensor.matmul_mx(
                         out=bank[:],
-                        lhsT=w_codes[:, P * m : P * m + P].bitcast(FP8X4),
-                        lhsT_scale=w_scales[:, P * m : P * m + P],
+                        lhsT=w_codes[m][:].bitcast(FP8X4),
+                        lhsT_scale=w_scales[m][:],
                         rhs=codes[s // HALF][:, s % HALF : s % HALF + BANK].bitcast(FP8X4),
                         rhs_scale=planes[s // HALF][:, s % HALF : s % HALF + BANK],
                         start=True,

@@ -17,6 +17,7 @@ MULT = mybir.AluOpType.mult
 
 HALF = 1024
 BANK = 512
+SHARE = 1280
 
 
 def tile_list_tabhs_gelu_kernel(tc, tab, w, b, wgo, offs, offs2, out):
@@ -24,12 +25,13 @@ def tile_list_tabhs_gelu_kernel(tc, tab, w, b, wgo, offs, offs2, out):
     with (
         tc.tile_pool(name="keep", bufs=1) as keep,
         tc.tile_pool(name="load", bufs=1) as load,
+        tc.tile_pool(name="wide", bufs=1) as wide,
         tc.psum_pool(name="psum", bufs=1) as psum,
     ):
         idx = keep.tile([P, S // 16], U16, name="idx")
         idx2 = keep.tile([P, S // 16], U16, name="idx2")
         rows = keep.tile([P, T], U8, name="rows", align_bytes=64)
-        seed = keep.tile([P, 32], F32, tag="wide", name="seed", align_bytes=64)
+        seed = wide.tile([P, 32], F32, name="seed", align_bytes=64, offset=4 * T - 64)
         zero = keep.tile([P, 32], F32, tag="first", name="zero", align_bytes=64)
         warm = load.tile([P, 32], F32, name="warm", align_bytes=64, offset=16 * M - 64)
         planes = [keep.tile([P, HALF], U8, name="plane%d" % h, align_bytes=64) for h in range(2)]
@@ -37,13 +39,15 @@ def tile_list_tabhs_gelu_kernel(tc, tab, w, b, wgo, offs, offs2, out):
         nc.vector.memset(seed[:], 0.0)
         nc.vector.memset(rows[:].bitcast(I32), 0)
         nc.vector.tensor_copy(zero[:], seed[:])
-        window1 = keep.tile([P, T], F32, name="window1", align_bytes=64)
-        nc.vector.memset(window1[:], 0.0)
+        window1 = wide.tile([P, T], F32, name="window1", align_bytes=64, offset=4 * T)
+        nc.vector.memset(window1[:, 0 : SHARE // 2 - 1], 0.0)
+        nc.vector.memset(window1[:, SHARE // 2 - 1 : SHARE], 0.0)
+        nc.gpsimd.memset(window1[:, SHARE:T], 0.0)
         nc.sync.dma_start(idx[:], offs)
         scale_rows = tab[0, 512 * T : 528 * T].rearrange("(q t) -> q t", t=T)
         nc.sync.dma_start(rows[0:P:8, :].bitcast(I32), scale_rows.bitcast(I32))
         nc.scalar.activation(warm[:], zero[:], GELU)
-        words = keep.tile([P, T], I32, tag="wide", name="words", align_bytes=64)
+        words = wide.tile([P, T], I32, name="words", align_bytes=64, offset=0)
         nc.sync.dma_start(words[:], tab[0, 0 : 512 * T].rearrange("(p c) -> p c", p=P).bitcast(I32))
         w_raw = load.tile([P, 4, M], F32, name="w_raw", align_bytes=64, offset=0)
         bias = load.tile([P, 2], F32, name="bias", align_bytes=64, offset=16 * M)
@@ -96,7 +100,7 @@ def tile_list_tabhs_gelu_kernel(tc, tab, w, b, wgo, offs, offs2, out):
         quantize(w_codes1, 1)
         w_codes = [w_codes0, w_codes1]
 
-        factor1 = keep.tile([P, S - BANK], F32, tag="wide", name="factor1", align_bytes=64)
+        factor1 = wide.tile([P, S - BANK], F32, name="factor1", align_bytes=64, offset=0)
         nc.sync.dma_start(factor1[:], wgo[:, BANK:S])
         factors = [factor0, factor1]
         windows = [window0, window1]

@@ -17,53 +17,53 @@ MULT = mybir.AluOpType.mult
 
 HALF = 1024
 BANK = 512
-SHARE = 1280
+LIVE = 112
+SHARE = 768
 
 
 def tile_list_tabhs_gelu_kernel(tc, tab, w, b, wgo, offs, offs2, out):
     nc = tc.nc
     with (
         tc.tile_pool(name="keep", bufs=1) as keep,
-        tc.tile_pool(name="load", bufs=1) as load,
-        tc.tile_pool(name="wide", bufs=1) as wide,
         tc.psum_pool(name="psum", bufs=1) as psum,
     ):
         idx = keep.tile([P, S // 16], U16, name="idx")
         idx2 = keep.tile([P, S // 16], U16, name="idx2")
         rows = keep.tile([P, T], U8, name="rows", align_bytes=64)
-        seed = wide.tile([P, 32], F32, name="seed", align_bytes=64, offset=4 * T - 64)
-        zero = keep.tile([P, 32], F32, tag="first", name="zero", align_bytes=64)
-        warm = load.tile([P, 32], F32, name="warm", align_bytes=64, offset=16 * M - 64)
+        words = keep.tile([P, T], I32, tag="wide", name="words", align_bytes=64)
+        w_raw = keep.tile([P, 4, M], F32, tag="load", name="w_raw", align_bytes=64)
+        bias = keep.tile([P, 2], F32, name="bias")
+        zero = keep.tile([P, 1], F32, name="zero")
+        warm = keep.tile([P, 1], F32, name="warm")
+        window0 = keep.tile([P, T], F32, name="window0", align_bytes=64)
+        window1 = keep.tile([P, T], F32, name="window1", align_bytes=64)
         planes = [keep.tile([P, HALF], U8, name="plane%d" % h, align_bytes=64) for h in range(2)]
 
-        nc.vector.memset(seed[:], 0.0)
-        nc.vector.memset(rows[:].bitcast(I32), 0)
-        nc.vector.tensor_copy(zero[:], seed[:])
-        window1 = wide.tile([P, T], F32, name="window1", align_bytes=64, offset=4 * T)
-        nc.vector.memset(window1[:, 0 : SHARE // 2 - 1], 0.0)
-        nc.vector.memset(window1[:, SHARE // 2 - 1 : SHARE], 0.0)
-        nc.gpsimd.memset(window1[:, SHARE:T], 0.0)
         nc.sync.dma_start(idx[:], offs)
         scale_rows = tab[0, 512 * T : 528 * T].rearrange("(q t) -> q t", t=T)
-        nc.sync.dma_start(rows[0:P:8, :].bitcast(I32), scale_rows.bitcast(I32))
-        nc.scalar.activation(warm[:], zero[:], GELU)
-        words = wide.tile([P, T], I32, name="words", align_bytes=64, offset=0)
+        nc.sync.dma_start(rows[LIVE:P, :].bitcast(I32), scale_rows.bitcast(I32))
         nc.sync.dma_start(words[:], tab[0, 0 : 512 * T].rearrange("(p c) -> p c", p=P).bitcast(I32))
-        w_raw = load.tile([P, 4, M], F32, name="w_raw", align_bytes=64, offset=0)
-        bias = load.tile([P, 2], F32, name="bias", align_bytes=64, offset=16 * M)
         nc.sync.dma_start(w_raw[:], w.rearrange("(p j) n -> p j n", j=4))
         with nc.allow_non_contiguous_dma(reason="256 values, one to a partition"):
             nc.sync.dma_start(bias[:], b.rearrange("(c p) -> p c", p=P))
         nc.sync.dma_start(idx2[:], offs2)
 
-        window0 = keep.tile([P, T], F32, tag="first", name="window0", align_bytes=64)
+        def clear(ap, n, value):
+            nc.vector.memset(ap[:, 0 : n // 2 - 1], value)
+            nc.vector.memset(ap[:, n // 2 - 1 : n], value)
+
+        nc.vector.memset(zero[:], 0.0)
+        nc.scalar.activation(warm[:], zero[:], GELU)
+        clear(rows[0:LIVE, :].bitcast(I32), T // 4, 0)
+        clear(window1[:], SHARE, 0.0)
         nc.gpsimd.memset(window0[:], 0.0)
+        nc.gpsimd.memset(window1[:, SHARE:T], 0.0)
 
         for h in range(2):
             picked = keep.tile([P, HALF], U8, tag="picked%d" % h, name="picked%d" % h, align_bytes=64)
             nc.vector.tensor_copy(picked[:], rows[:].indirect(idx[:, h * HALF // 16 : (h + 1) * HALF // 16]))
             for r in range(4):
-                nc.sync.dma_start(planes[h][r:P:32, :].bitcast(I32), picked[8 * r : P : 32, :].bitcast(I32))
+                nc.sync.dma_start(planes[h][r:P:32, :].bitcast(I32), picked[LIVE + r : P : 4, :].bitcast(I32))
 
         factor0 = keep.tile([P, BANK], F32, tag="picked0", name="factor0", align_bytes=64)
         nc.sync.dma_start(factor0[:], wgo[:, 0:BANK])
@@ -93,14 +93,14 @@ def tile_list_tabhs_gelu_kernel(tc, tab, w, b, wgo, offs, offs2, out):
         gather_words(codes0, 0)
         w_codes0 = keep.tile([P, P], U32, name="w_codes0", align_bytes=64)
         quantize(w_codes0, 0)
-        codes1 = load.tile([P, HALF], U32, name="codes1", align_bytes=64, offset=0)
+        codes1 = keep.tile([P, HALF], U32, tag="load", name="codes1", align_bytes=64)
         gather_words(codes1, 1)
         codes = [codes0, codes1]
         w_codes1 = keep.tile([P, P], U32, tag="late", name="w_codes1", align_bytes=64)
         quantize(w_codes1, 1)
         w_codes = [w_codes0, w_codes1]
 
-        factor1 = wide.tile([P, S - BANK], F32, name="factor1", align_bytes=64, offset=0)
+        factor1 = keep.tile([P, S - BANK], F32, tag="wide", name="factor1", align_bytes=64)
         nc.sync.dma_start(factor1[:], wgo[:, BANK:S])
         factors = [factor0, factor1]
         windows = [window0, window1]

@@ -31,7 +31,10 @@ def tile_list_tabhs_gelu_kernel(tc, tab, w, b, wgo, offs, offs2, out):
         idx2 = keep.tile([P, S // 16], U16, name="idx2")
         rows = keep.tile([P, T], U8, name="rows", align_bytes=64)
         words = keep.tile([P, T], I32, tag="wide", name="words", align_bytes=64)
-        w_raw = keep.tile([P, 4, M], F32, tag="load", name="w_raw", align_bytes=64)
+        w_raw = [
+            keep.tile([P, 4, P], F32, tag="load", name="w_raw0", align_bytes=64),
+            keep.tile([P, 4, P], F32, name="w_raw1", align_bytes=64),
+        ]
         bias = keep.tile([P, 2], F32, name="bias")
         zero = keep.tile([P, 1], F32, name="zero")
         warm = keep.tile([P, 1], F32, name="warm")
@@ -43,7 +46,8 @@ def tile_list_tabhs_gelu_kernel(tc, tab, w, b, wgo, offs, offs2, out):
         scale_rows = tab[0, 512 * T : 528 * T].rearrange("(q t) -> q t", t=T)
         nc.sync.dma_start(rows[LIVE:P, :].bitcast(I32), scale_rows.bitcast(I32))
         nc.sync.dma_start(words[:], tab[0, 0 : 512 * T].rearrange("(p c) -> p c", p=P).bitcast(I32))
-        nc.sync.dma_start(w_raw[:], w.rearrange("(p j) n -> p j n", j=4))
+        for m in range(2):
+            nc.sync.dma_start(w_raw[m][:], w[:, P * m : P * m + P].rearrange("(p j) n -> p j n", j=4))
         with nc.allow_non_contiguous_dma(reason="256 values, one to a partition"):
             nc.sync.dma_start(bias[:], b.rearrange("(c p) -> p c", p=P))
         nc.sync.dma_start(idx2[:], offs2)
@@ -73,7 +77,7 @@ def tile_list_tabhs_gelu_kernel(tc, tab, w, b, wgo, offs, offs2, out):
             keep.tile([P, P, 4], BF16, name="group1", align_bytes=64),
         ]
         for m in range(2):
-            nc.scalar.activation(groups[m][:], w_raw[:, :, P * m : P * m + P].rearrange("p j n -> p n j"), COPY)
+            nc.scalar.activation(groups[m][:], w_raw[m][:].rearrange("p j n -> p n j"), COPY)
         w_scales = [keep.tile([P, P], U8, name="w_scales%d" % m, align_bytes=64) for m in range(2)]
 
         def quantize(w_codes, m):

@@ -36,8 +36,6 @@ def tile_list_tabhs_gelu_kernel(tc, tab, w, b, wgo, offs, offs2, out):
             keep.tile([P, 4, P], F32, name="w_raw1", align_bytes=64),
         ]
         bias = keep.tile([P, 2], F32, name="bias")
-        zero = keep.tile([P, 1], F32, name="zero")
-        warm = keep.tile([P, 1], F32, name="warm")
         window0 = keep.tile([P, T], F32, name="window0", align_bytes=64)
         window1 = keep.tile([P, T], F32, name="window1", align_bytes=64)
         planes = [keep.tile([P, HALF], U8, name="plane%d" % h, align_bytes=64) for h in range(2)]
@@ -56,8 +54,6 @@ def tile_list_tabhs_gelu_kernel(tc, tab, w, b, wgo, offs, offs2, out):
             nc.vector.memset(ap[:, 0 : n // 2 - 1], value)
             nc.vector.memset(ap[:, n // 2 - 1 : n], value)
 
-        nc.vector.memset(zero[:], 0.0)
-        nc.scalar.activation(warm[:], zero[:], GELU)
         clear(rows[0:LIVE, :].bitcast(I32), T // 4, 0)
         clear(window1[:], SHARE, 0.0)
         nc.gpsimd.memset(window0[:], 0.0)

@@ -29,7 +29,7 @@ def tile_list_tabhs_gelu_kernel(tc, tab, w, b, wgo, offs, offs2, out):
     ):
         idx = keep.tile([P, S // 16], U16, name="idx")
         idx2 = keep.tile([P, S // 16], U16, name="idx2")
-        rows = keep.tile([P, T], U8, name="rows", align_bytes=64)
+        rows = keep.tile([P, T], U8, tag="rows", name="rows", align_bytes=64)
         words = keep.tile([P, T], I32, tag="wide", name="words", align_bytes=64)
         w_raw = [
             keep.tile([P, 4, P], F32, tag="load", name="w_raw0", align_bytes=64),
@@ -38,7 +38,7 @@ def tile_list_tabhs_gelu_kernel(tc, tab, w, b, wgo, offs, offs2, out):
         bias = keep.tile([P, 2], F32, name="bias")
         window0 = keep.tile([P, T], F32, name="window0", align_bytes=64)
         window1 = keep.tile([P, T], F32, name="window1", align_bytes=64)
-        planes = [keep.tile([P, HALF], U8, name="plane%d" % h, align_bytes=64) for h in range(2)]
+        plane = keep.tile([P, S], U8, name="plane", align_bytes=64)
 
         nc.sync.dma_start(idx[:], offs)
         scale_rows = tab[0, 512 * T : 528 * T].rearrange("(q t) -> q t", t=T)
@@ -59,13 +59,12 @@ def tile_list_tabhs_gelu_kernel(tc, tab, w, b, wgo, offs, offs2, out):
         nc.gpsimd.memset(window0[:], 0.0)
         nc.gpsimd.memset(window1[:, SHARE:T], 0.0)
 
-        for h in range(2):
-            picked = keep.tile([P, HALF], U8, tag="picked%d" % h, name="picked%d" % h, align_bytes=64)
-            nc.vector.tensor_copy(picked[:], rows[:].indirect(idx[:, h * HALF // 16 : (h + 1) * HALF // 16]))
-            for r in range(4):
-                nc.sync.dma_start(planes[h][r:P:32, :].bitcast(I32), picked[LIVE + r : P : 4, :].bitcast(I32))
+        picked = keep.tile([P, S], U8, name="picked", align_bytes=64)
+        nc.vector.tensor_copy(picked[:], rows[:].indirect(idx[:]))
+        for r in range(4):
+            nc.sync.dma_start(plane[r:P:32, :].bitcast(I32), picked[LIVE + r : P : 4, :].bitcast(I32))
 
-        factor0 = keep.tile([P, BANK], F32, tag="picked0", name="factor0", align_bytes=64)
+        factor0 = keep.tile([P, BANK], F32, tag="rows", name="factor0", align_bytes=64)
         nc.sync.dma_start(factor0[:], wgo[:, 0:BANK])
 
         groups = [
@@ -114,7 +113,7 @@ def tile_list_tabhs_gelu_kernel(tc, tab, w, b, wgo, offs, offs2, out):
                         lhsT=w_codes[m][:].bitcast(FP8X4),
                         lhsT_scale=w_scales[m][:],
                         rhs=codes[s // HALF][:, s % HALF : s % HALF + BANK].bitcast(FP8X4),
-                        rhs_scale=planes[s // HALF][:, s % HALF : s % HALF + BANK],
+                        rhs_scale=plane[:, s : s + BANK],
                         start=True,
                         stop=True,
                     )

@@ -40,9 +40,9 @@ def tile_list_tabhs_gelu_kernel(tc, tab, w, b, wgo, offs, offs2, out):
         window1 = keep.tile([P, T], F32, name="window1", align_bytes=64)
         plane = keep.tile([P, S], U8, name="plane", align_bytes=64)
 
-        nc.sync.dma_start(idx[:], offs)
         scale_rows = tab[0, 512 * T : 528 * T].rearrange("(q t) -> q t", t=T)
         nc.sync.dma_start(rows[LIVE:P, :].bitcast(I32), scale_rows.bitcast(I32))
+        nc.sync.dma_start(idx[:], offs)
         nc.sync.dma_start(words[:], tab[0, 0 : 512 * T].rearrange("(p c) -> p c", p=P).bitcast(I32))
         for m in range(2):
             nc.sync.dma_start(w_raw[m][:], w[:, P * m : P * m + P].rearrange("(p j) n -> p j n", j=4))

@@ -14,6 +14,7 @@ FP8X4 = mybir.dt.float8_e4m3fn_x4
 COPY = mybir.ActivationFunctionType.Copy
 GELU = mybir.ActivationFunctionType.Gelu_apprx_tanh
 MULT = mybir.AluOpType.mult
+ADD = mybir.AluOpType.add
 
 HALF = 1024
 BANK = 512
@@ -31,11 +32,8 @@ def tile_list_tabhs_gelu_kernel(tc, tab, w, b, wgo, offs, offs2, out):
         idx2 = keep.tile([P, S // 16], U16, name="idx2")
         rows = keep.tile([P, T], U8, tag="rows", name="rows", align_bytes=64)
         words = keep.tile([P, T], I32, tag="wide", name="words", align_bytes=64)
-        w_raw = [
-            keep.tile([P, 4, P], F32, tag="load", name="w_raw0", align_bytes=64),
-            keep.tile([P, 4, P], F32, name="w_raw1", align_bytes=64),
-        ]
-        bias = keep.tile([P, 2], F32, name="bias")
+        w_raw = keep.tile([P, 4, M], F32, tag="load", name="w_raw", align_bytes=64)
+        bias = [keep.tile([P, 1], F32, name="bias%d" % m) for m in range(2)]
         window0 = keep.tile([P, T], F32, name="window0", align_bytes=64)
         window1 = keep.tile([P, T], F32, name="window1", align_bytes=64)
         plane = keep.tile([P, S], U8, name="plane", align_bytes=64)
@@ -44,10 +42,10 @@ def tile_list_tabhs_gelu_kernel(tc, tab, w, b, wgo, offs, offs2, out):
         nc.sync.dma_start(rows[LIVE:P, :].bitcast(I32), scale_rows.bitcast(I32))
         nc.sync.dma_start(idx[:], offs)
         nc.sync.dma_start(words[:], tab[0, 0 : 512 * T].rearrange("(p c) -> p c", p=P).bitcast(I32))
-        for m in range(2):
-            nc.sync.dma_start(w_raw[m][:], w[:, P * m : P * m + P].rearrange("(p j) n -> p j n", j=4))
+        nc.sync.dma_start(w_raw[:], w.rearrange("(p j) n -> p j n", j=4))
         with nc.allow_non_contiguous_dma(reason="256 values, one to a partition"):
-            nc.sync.dma_start(bias[:], b.rearrange("(c p) -> p c", p=P))
+            for m in range(2):
+                nc.sync.dma_start(bias[m][:], b[P * m : P * m + P].rearrange("(p c) -> p c", c=1))
         nc.sync.dma_start(idx2[:], offs2)
 
         def clear(ap, n, value):
@@ -67,20 +65,12 @@ def tile_list_tabhs_gelu_kernel(tc, tab, w, b, wgo, offs, offs2, out):
         factor0 = keep.tile([P, BANK], F32, tag="rows", name="factor0", align_bytes=64)
         nc.sync.dma_start(factor0[:], wgo[:, 0:BANK])
 
-        groups = [
-            keep.tile([P, P, 4], BF16, tag="late", name="group0", align_bytes=64),
-            keep.tile([P, P, 4], BF16, name="group1", align_bytes=64),
-        ]
-        for m in range(2):
-            nc.scalar.activation(groups[m][:], w_raw[m][:].rearrange("p j n -> p n j"), COPY)
-        w_scales = [keep.tile([P, P], U8, name="w_scales%d" % m, align_bytes=64) for m in range(2)]
-
-        def quantize(w_codes, m):
-            nc.vector.quantize_mx(
-                out=w_codes[:].bitcast(FP8X4),
-                scales=w_scales[m][:],
-                in_=groups[m][:].rearrange("p n j -> p (n j)"),
-            )
+        group = keep.tile([P, M, 4], BF16, name="group", align_bytes=64)
+        columns = w_raw[:].rearrange("p j n -> p n j")
+        nc.scalar.activation(group[:, 0:P, :], columns[:, 0:P, :], COPY)
+        nc.gpsimd.tensor_scalar(group[:, P:M, :], columns[:, P:M, :], 1.0, 0.0, MULT, ADD)
+        w_scales = keep.tile([P, M], U8, name="w_scales", align_bytes=64)
+        w_codes = keep.tile([P, M], U32, name="w_codes", align_bytes=64)
 
         def gather_words(codes, h):
             nc.vector.tensor_copy(
@@ -90,14 +80,14 @@ def tile_list_tabhs_gelu_kernel(tc, tab, w, b, wgo, offs, offs2, out):
 
         codes0 = keep.tile([P, HALF], U32, name="codes0", align_bytes=64)
         gather_words(codes0, 0)
-        w_codes0 = keep.tile([P, P], U32, name="w_codes0", align_bytes=64)
-        quantize(w_codes0, 0)
+        nc.vector.quantize_mx(
+            out=w_codes[:].bitcast(FP8X4),
+            scales=w_scales[:],
+            in_=group[:].rearrange("p n j -> p (n j)"),
+        )
         codes1 = keep.tile([P, HALF], U32, tag="load", name="codes1", align_bytes=64)
         gather_words(codes1, 1)
         codes = [codes0, codes1]
-        w_codes1 = keep.tile([P, P], U32, tag="late", name="w_codes1", align_bytes=64)
-        quantize(w_codes1, 1)
-        w_codes = [w_codes0, w_codes1]
 
         factor1 = keep.tile([P, S - BANK], F32, tag="wide", name="factor1", align_bytes=64)
         nc.sync.dma_start(factor1[:], wgo[:, BANK:S])
@@ -110,14 +100,14 @@ def tile_list_tabhs_gelu_kernel(tc, tab, w, b, wgo, offs, offs2, out):
                     bank = psum.tile([P, BANK], F32, name="bank%d_%d" % (m, s // BANK))
                     nc.tensor.matmul_mx(
                         out=bank[:],
-                        lhsT=w_codes[m][:].bitcast(FP8X4),
-                        lhsT_scale=w_scales[m][:],
+                        lhsT=w_codes[:, P * m : P * m + P].bitcast(FP8X4),
+                        lhsT_scale=w_scales[:, P * m : P * m + P],
                         rhs=codes[s // HALF][:, s % HALF : s % HALF + BANK].bitcast(FP8X4),
                         rhs_scale=plane[:, s : s + BANK],
                         start=True,
                         stop=True,
                     )
-                    nc.scalar.activation(y[m][:, s : s + BANK], bank[:], GELU, bias=bias[:, m : m + 1])
+                    nc.scalar.activation(y[m][:, s : s + BANK], bank[:], GELU, bias=bias[m][:])
                 nc.vector.tensor_tensor(
                     windows[m][:].indirect(idx2[:, lo // 16 : hi // 16]),
                     y[m][:, lo:hi],

@@ -20,6 +20,7 @@ HALF = 1024
 BANK = 512
 LIVE = 112
 SHARE = 768
+LAST = 768
 
 
 def tile_list_tabhs_gelu_kernel(tc, tab, w, b, wgo, offs, offs2, out):
@@ -91,28 +92,34 @@ def tile_list_tabhs_gelu_kernel(tc, tab, w, b, wgo, offs, offs2, out):
 
         factor1 = keep.tile([P, S - BANK], F32, tag="wide", name="factor1", align_bytes=64)
         nc.sync.dma_start(factor1[:], wgo[:, BANK:S])
-        factors = [factor0, factor1]
         windows = [window0, window1]
         y = [keep.tile([P, S], F32, name="y%d" % m) for m in range(2)]
-        for (lo, hi), factor in zip(((0, BANK), (BANK, S)), factors):
-            for m in range(2):
-                for s in range(lo, hi, BANK):
-                    bank = psum.tile([P, BANK], F32, name="bank%d_%d" % (m, s // BANK))
-                    nc.tensor.matmul_mx(
-                        out=bank[:],
-                        lhsT=w_codes[:, P * m : P * m + P].bitcast(FP8X4),
-                        lhsT_scale=w_scales[:, P * m : P * m + P],
-                        rhs=codes[s // HALF][:, s % HALF : s % HALF + BANK].bitcast(FP8X4),
-                        rhs_scale=plane[:, s : s + BANK],
-                        start=True,
-                        stop=True,
-                    )
-                    nc.scalar.activation(y[m][:, s : s + BANK], bank[:], GELU, bias=bias[m][:])
-                nc.vector.tensor_tensor(
-                    windows[m][:].indirect(idx2[:, lo // 16 : hi // 16]),
-                    y[m][:, lo:hi],
-                    factor[:],
-                    MULT,
-                )
+
+        def project(m, s):
+            bank = psum.tile([P, BANK], F32, name="bank%d_%d" % (m, s // BANK))
+            nc.tensor.matmul_mx(
+                out=bank[:],
+                lhsT=w_codes[:, P * m : P * m + P].bitcast(FP8X4),
+                lhsT_scale=w_scales[:, P * m : P * m + P],
+                rhs=codes[s // HALF][:, s % HALF : s % HALF + BANK].bitcast(FP8X4),
+                rhs_scale=plane[:, s : s + BANK],
+                start=True,
+                stop=True,
+            )
+            nc.scalar.activation(y[m][:, s : s + BANK], bank[:], GELU, bias=bias[m][:])
+
+        def place(m, lo, hi):
+            factor = factor0[:, lo:hi] if hi <= BANK else factor1[:, lo - BANK : hi - BANK]
+            nc.vector.tensor_tensor(windows[m][:].indirect(idx2[:, lo // 16 : hi // 16]), y[m][:, lo:hi], factor, MULT)
+
+        for m in (1, 0):
+            project(m, 0)
+            place(m, 0, BANK)
+        for m in (1, 0):
+            for s in range(BANK, S, BANK):
+                project(m, s)
+        place(1, BANK, S - LAST)
+        place(0, BANK, S)
+        place(1, S - LAST, S)
         for m in range(2):
             nc.sync.dma_start(out[P * m : P * m + P, :], windows[m][:])

@@ -19,7 +19,7 @@ ADD = mybir.AluOpType.add
 HALF = 1024
 BANK = 512
 LIVE = 112
-SHARE = 768
+SHARE = 1792
 LAST = 768
 
 
@@ -53,7 +53,7 @@ def tile_list_tabhs_gelu_kernel(tc, tab, w, b, wgo, offs, offs2, out):
             nc.vector.memset(ap[:, 0 : n // 2 - 1], value)
             nc.vector.memset(ap[:, n // 2 - 1 : n], value)
 
-        clear(rows[0:LIVE, :].bitcast(I32), T // 4, 0)
+        nc.gpsimd.memset(rows[0:LIVE, :].bitcast(I32), 0)
         clear(window1[:], SHARE, 0.0)
         nc.gpsimd.memset(window0[:], 0.0)
         nc.gpsimd.memset(window1[:, SHARE:T], 0.0)

@@ -29,15 +29,15 @@ def tile_list_tabhs_gelu_kernel(tc, tab, w, b, wgo, offs, offs2, out):
         tc.tile_pool(name="keep", bufs=1) as keep,
         tc.psum_pool(name="psum", bufs=1) as psum,
     ):
-        idx = keep.tile([P, S // 16], U16, name="idx")
-        idx2 = keep.tile([P, S // 16], U16, name="idx2")
-        rows = keep.tile([P, T], U8, tag="rows", name="rows", align_bytes=64)
-        words = keep.tile([P, T], I32, tag="wide", name="words", align_bytes=64)
-        w_raw = keep.tile([P, 4, M], F32, tag="load", name="w_raw", align_bytes=64)
+        idx = keep.tile([P, S // 16], U16, name="idx", align_bytes=256)
+        idx2 = keep.tile([P, S // 16], U16, name="idx2", align_bytes=256)
+        rows = keep.tile([P, T], U8, tag="rows", name="rows", align_bytes=256)
+        words = keep.tile([P, T], I32, tag="wide", name="words", align_bytes=256)
+        w_raw = keep.tile([P, 4, M], F32, tag="load", name="w_raw", align_bytes=256)
         bias = [keep.tile([P, 1], F32, name="bias%d" % m) for m in range(2)]
-        window0 = keep.tile([P, T], F32, name="window0", align_bytes=64)
-        window1 = keep.tile([P, T], F32, name="window1", align_bytes=64)
-        plane = keep.tile([P, S], U8, name="plane", align_bytes=64)
+        window0 = keep.tile([P, T], F32, name="window0", align_bytes=256)
+        window1 = keep.tile([P, T], F32, name="window1", align_bytes=256)
+        plane = keep.tile([P, S], U8, name="plane", align_bytes=256)
 
         scale_rows = tab[0, 512 * T : 528 * T].rearrange("(q t) -> q t", t=T)
         nc.sync.dma_start(rows[LIVE:P, :].bitcast(I32), scale_rows.bitcast(I32))
@@ -58,20 +58,20 @@ def tile_list_tabhs_gelu_kernel(tc, tab, w, b, wgo, offs, offs2, out):
         nc.gpsimd.memset(window0[:], 0.0)
         nc.gpsimd.memset(window1[:, SHARE:T], 0.0)
 
-        picked = keep.tile([P, S], U8, name="picked", align_bytes=64)
+        picked = keep.tile([P, S], U8, name="picked", align_bytes=256)
         nc.vector.tensor_copy(picked[:], rows[:].indirect(idx[:]))
         for r in range(4):
             nc.sync.dma_start(plane[r:P:32, :].bitcast(I32), picked[LIVE + r : P : 4, :].bitcast(I32))
 
-        factor0 = keep.tile([P, BANK], F32, tag="rows", name="factor0", align_bytes=64)
+        factor0 = keep.tile([P, BANK], F32, tag="rows", name="factor0", align_bytes=256)
         nc.sync.dma_start(factor0[:], wgo[:, 0:BANK])
 
-        group = keep.tile([P, M, 4], BF16, name="group", align_bytes=64)
+        group = keep.tile([P, M, 4], BF16, name="group", align_bytes=256)
         columns = w_raw[:].rearrange("p j n -> p n j")
         nc.scalar.activation(group[:, 0:P, :], columns[:, 0:P, :], COPY)
         nc.gpsimd.tensor_scalar(group[:, P:M, :], columns[:, P:M, :], 1.0, 0.0, MULT, ADD)
-        w_scales = keep.tile([P, M], U8, name="w_scales", align_bytes=64)
-        w_codes = keep.tile([P, M], U32, name="w_codes", align_bytes=64)
+        w_scales = keep.tile([P, M], U8, name="w_scales", align_bytes=256)
+        w_codes = keep.tile([P, M], U32, name="w_codes", align_bytes=256)
 
         def gather_words(codes, h):
             nc.vector.tensor_copy(
@@ -79,21 +79,21 @@ def tile_list_tabhs_gelu_kernel(tc, tab, w, b, wgo, offs, offs2, out):
                 words[:].bitcast(U32).indirect(idx[:, h * HALF // 16 : (h + 1) * HALF // 16]),
             )
 
-        codes0 = keep.tile([P, HALF], U32, name="codes0", align_bytes=64)
+        codes0 = keep.tile([P, HALF], U32, name="codes0", align_bytes=256)
         gather_words(codes0, 0)
         nc.vector.quantize_mx(
             out=w_codes[:].bitcast(FP8X4),
             scales=w_scales[:],
             in_=group[:].rearrange("p n j -> p (n j)"),
         )
-        codes1 = keep.tile([P, HALF], U32, tag="load", name="codes1", align_bytes=64)
+        codes1 = keep.tile([P, HALF], U32, tag="load", name="codes1", align_bytes=256)
         gather_words(codes1, 1)
         codes = [codes0, codes1]
 
-        factor1 = keep.tile([P, S - BANK], F32, tag="wide", name="factor1", align_bytes=64)
+        factor1 = keep.tile([P, S - BANK], F32, tag="wide", name="factor1", align_bytes=256)
         nc.sync.dma_start(factor1[:], wgo[:, BANK:S])
         windows = [window0, window1]
-        y = [keep.tile([P, S], F32, name="y%d" % m) for m in range(2)]
+        y = [keep.tile([P, S], F32, name="y%d" % m, align_bytes=256) for m in range(2)]
 
         def project(m, s):
             bank = psum.tile([P, BANK], F32, name="bank%d_%d" % (m, s // BANK))

@@ -21,6 +21,7 @@ BANK = 512
 LIVE = 112
 SHARE = 1792
 LAST = 768
+SPLIT = 40
 
 
 def tile_list_tabhs_gelu_kernel(tc, tab, w, b, wgo, offs, offs2, out):
@@ -67,9 +68,11 @@ def tile_list_tabhs_gelu_kernel(tc, tab, w, b, wgo, offs, offs2, out):
         nc.sync.dma_start(factor0[:], wgo[:, 0:BANK])
 
         group = keep.tile([P, M, 4], BF16, name="group", align_bytes=256)
+        cast_out = group[:].rearrange("p (c i) j -> p c j i", i=4)
+        cast_in = w_raw[:].rearrange("p j (c i) -> p c j i", i=4)
+        nc.scalar.activation(cast_out[:, 0:SPLIT], cast_in[:, 0:SPLIT], COPY)
         columns = w_raw[:].rearrange("p j n -> p n j")
-        nc.scalar.activation(group[:, 0:P, :], columns[:, 0:P, :], COPY)
-        nc.gpsimd.tensor_scalar(group[:, P:M, :], columns[:, P:M, :], 1.0, 0.0, MULT, ADD)
+        nc.gpsimd.tensor_scalar(group[:, 4 * SPLIT : M, :], columns[:, 4 * SPLIT : M, :], 1.0, 0.0, MULT, ADD)
         w_scales = keep.tile([P, M], U8, name="w_scales", align_bytes=256)
         w_codes = keep.tile([P, M], U32, name="w_codes", align_bytes=256)
 

@@ -14,14 +14,14 @@ FP8X4 = mybir.dt.float8_e4m3fn_x4
 COPY = mybir.ActivationFunctionType.Copy
 GELU = mybir.ActivationFunctionType.Gelu_apprx_tanh
 MULT = mybir.AluOpType.mult
-ADD = mybir.AluOpType.add
 
-HALF = 1024
+RING = 768
 BANK = 512
+STEP = 256
+LATE = S - RING
 LIVE = 112
 SHARE = 1792
 LAST = 768
-SPLIT = 40
 
 
 def tile_list_tabhs_gelu_kernel(tc, tab, w, b, wgo, offs, offs2, out):
@@ -34,20 +34,20 @@ def tile_list_tabhs_gelu_kernel(tc, tab, w, b, wgo, offs, offs2, out):
         idx2 = keep.tile([P, S // 16], U16, name="idx2", align_bytes=256)
         rows = keep.tile([P, T], U8, tag="rows", name="rows", align_bytes=256)
         words = keep.tile([P, T], I32, tag="wide", name="words", align_bytes=256)
-        w_raw = keep.tile([P, 4, M], F32, tag="load", name="w_raw", align_bytes=256)
-        bias = [keep.tile([P, 1], F32, name="bias%d" % m) for m in range(2)]
+        w_raw = [keep.tile([P, 4, P], F32, tag="load%d" % m, name="w_raw%d" % m, align_bytes=256) for m in range(2)]
+        bias = keep.tile([P, 2], F32, name="bias")
         window0 = keep.tile([P, T], F32, name="window0", align_bytes=256)
         window1 = keep.tile([P, T], F32, name="window1", align_bytes=256)
-        plane = keep.tile([P, S], U8, name="plane", align_bytes=256)
+        planes = [keep.tile([P, n], U8, name="plane%d" % n, align_bytes=256) for n in (RING, S - RING)]
 
         scale_rows = tab[0, 512 * T : 528 * T].rearrange("(q t) -> q t", t=T)
         nc.sync.dma_start(rows[LIVE:P, :].bitcast(I32), scale_rows.bitcast(I32))
         nc.sync.dma_start(idx[:], offs)
         nc.sync.dma_start(words[:], tab[0, 0 : 512 * T].rearrange("(p c) -> p c", p=P).bitcast(I32))
-        nc.sync.dma_start(w_raw[:], w.rearrange("(p j) n -> p j n", j=4))
+        for m in (1, 0):
+            nc.sync.dma_start(w_raw[m][:], w[:, P * m : P * m + P].rearrange("(p j) n -> p j n", j=4))
         with nc.allow_non_contiguous_dma(reason="256 values, one to a partition"):
-            for m in range(2):
-                nc.sync.dma_start(bias[m][:], b[P * m : P * m + P].rearrange("(p c) -> p c", c=1))
+            nc.sync.dma_start(bias[:], b.rearrange("(c p) -> p c", p=P))
         nc.sync.dma_start(idx2[:], offs2)
 
         def clear(ap, n, value):
@@ -59,70 +59,99 @@ def tile_list_tabhs_gelu_kernel(tc, tab, w, b, wgo, offs, offs2, out):
         nc.gpsimd.memset(window0[:], 0.0)
         nc.gpsimd.memset(window1[:, SHARE:T], 0.0)
 
-        picked = keep.tile([P, S], U8, name="picked", align_bytes=256)
-        nc.vector.tensor_copy(picked[:], rows[:].indirect(idx[:]))
-        for r in range(4):
-            nc.sync.dma_start(plane[r:P:32, :].bitcast(I32), picked[LIVE + r : P : 4, :].bitcast(I32))
+        warm = keep.tile([P, 16], F32, name="warm")
+        nc.vector.memset(warm[:, 0:1], 0.0)
+        nc.scalar.activation(warm[:, 8:9], warm[:, 0:1], GELU)
 
-        factor0 = keep.tile([P, BANK], F32, tag="rows", name="factor0", align_bytes=256)
-        nc.sync.dma_start(factor0[:], wgo[:, 0:BANK])
+        picked = [keep.tile([P, n], U8, name="picked%d" % n, align_bytes=256) for n in (RING, S - RING)]
 
-        group = keep.tile([P, M, 4], BF16, name="group", align_bytes=256)
-        cast_out = group[:].rearrange("p (c i) j -> p c j i", i=4)
-        cast_in = w_raw[:].rearrange("p j (c i) -> p c j i", i=4)
-        nc.scalar.activation(cast_out[:, 0:SPLIT], cast_in[:, 0:SPLIT], COPY)
-        columns = w_raw[:].rearrange("p j n -> p n j")
-        nc.gpsimd.tensor_scalar(group[:, 4 * SPLIT : M, :], columns[:, 4 * SPLIT : M, :], 1.0, 0.0, MULT, ADD)
-        w_scales = keep.tile([P, M], U8, name="w_scales", align_bytes=256)
-        w_codes = keep.tile([P, M], U32, name="w_codes", align_bytes=256)
+        def move_scales(i):
+            for r in range(4):
+                nc.sync.dma_start(planes[i][r:P:32, :].bitcast(I32), picked[i][LIVE + r : P : 4, :].bitcast(I32))
 
-        def gather_words(codes, h):
-            nc.vector.tensor_copy(
-                codes[:],
-                words[:].bitcast(U32).indirect(idx[:, h * HALF // 16 : (h + 1) * HALF // 16]),
+        nc.vector.tensor_copy(picked[0][:], rows[:].indirect(idx[:, 0 : RING // 16]))
+        move_scales(0)
+        nc.vector.tensor_copy(picked[1][:], rows[:].indirect(idx[:, RING // 16 : S // 16]))
+        factor0 = keep.tile([P, STEP], F32, tag="rows", name="factor0", align_bytes=256)
+        nc.sync.dma_start(factor0[:], wgo[:, 0:STEP])
+        move_scales(1)
+
+        group = [keep.tile([P, P, 4], BF16, tag="group%d" % m, name="group%d" % m, align_bytes=256) for m in range(2)]
+        w_scales = [keep.tile([P, P], U8, name="w_scales%d" % m, align_bytes=256) for m in range(2)]
+        w_codes = [keep.tile([P, P], U32, name="w_codes%d" % m, align_bytes=256) for m in range(2)]
+
+        def cast(m):
+            cast_out = group[m][:].rearrange("p (c i) j -> p c j i", i=4)
+            cast_in = w_raw[m][:].rearrange("p j (c i) -> p c j i", i=4)
+            nc.scalar.activation(cast_out, cast_in, COPY)
+
+        def quantise(m):
+            nc.vector.quantize_mx(
+                out=w_codes[m][:].bitcast(FP8X4),
+                scales=w_scales[m][:],
+                in_=group[m][:].rearrange("p n j -> p (n j)"),
             )
 
-        codes0 = keep.tile([P, HALF], U32, name="codes0", align_bytes=256)
-        gather_words(codes0, 0)
-        nc.vector.quantize_mx(
-            out=w_codes[:].bitcast(FP8X4),
-            scales=w_scales[:],
-            in_=group[:].rearrange("p n j -> p (n j)"),
-        )
-        codes1 = keep.tile([P, HALF], U32, tag="load", name="codes1", align_bytes=256)
-        gather_words(codes1, 1)
-        codes = [codes0, codes1]
+        def gather_words(dst, lo, hi):
+            nc.vector.tensor_copy(dst, words[:].bitcast(U32).indirect(idx[:, lo // 16 : hi // 16]))
 
-        factor1 = keep.tile([P, S - BANK], F32, tag="wide", name="factor1", align_bytes=256)
-        nc.sync.dma_start(factor1[:], wgo[:, BANK:S])
+        first = keep.tile([P, BANK], U32, name="first", align_bytes=256)
+        cast(1)
+        cast(0)
+        gather_words(first[:], 0, BANK)
+        quantise(1)
+        cover = keep.tile([P, LATE - BANK], U32, tag="load1", name="cover", align_bytes=256)
+        gather_words(cover[:], BANK, LATE)
+        quantise(0)
+
+        factor1 = keep.tile([P, S - STEP], F32, tag="group1", name="factor1", align_bytes=256)
+        nc.sync.dma_start(factor1[:], wgo[:, STEP:S])
         windows = [window0, window1]
         y = [keep.tile([P, S], F32, name="y%d" % m, align_bytes=256) for m in range(2)]
 
-        def project(m, s):
-            bank = psum.tile([P, BANK], F32, name="bank%d_%d" % (m, s // BANK))
+        def project(m, lo, codes, tag):
+            hi = lo + codes.shape[1]
+            bank = psum.tile([P, hi - lo], F32, tag=tag, name="bank%d_%d" % (m, lo))
             nc.tensor.matmul_mx(
                 out=bank[:],
-                lhsT=w_codes[:, P * m : P * m + P].bitcast(FP8X4),
-                lhsT_scale=w_scales[:, P * m : P * m + P],
-                rhs=codes[s // HALF][:, s % HALF : s % HALF + BANK].bitcast(FP8X4),
-                rhs_scale=plane[:, s : s + BANK],
+                lhsT=w_codes[m][:].bitcast(FP8X4),
+                lhsT_scale=w_scales[m][:],
+                rhs=codes.bitcast(FP8X4),
+                rhs_scale=planes[0][:, lo:hi] if lo < RING else planes[1][:, lo - RING : hi - RING],
                 start=True,
                 stop=True,
             )
-            nc.scalar.activation(y[m][:, s : s + BANK], bank[:], GELU, bias=bias[m][:])
+            nc.scalar.activation(y[m][:, lo:hi], bank[:], GELU, bias=bias[:, m : m + 1])
 
         def place(m, lo, hi):
-            factor = factor0[:, lo:hi] if hi <= BANK else factor1[:, lo - BANK : hi - BANK]
+            factor = factor0[:, lo:hi] if hi <= STEP else factor1[:, lo - STEP : hi - STEP]
             nc.vector.tensor_tensor(windows[m][:].indirect(idx2[:, lo // 16 : hi // 16]), y[m][:, lo:hi], factor, MULT)
 
+        def slot(i):
+            return first[:, i * STEP : (i + 1) * STEP] if i < 2 else cover[:, 0:STEP]
+
+        def refill(i):
+            gather_words(slot(i), LATE + i * STEP, LATE + (i + 1) * STEP)
+
+        project(1, 0, slot(0), "turn")
+        place(1, 0, STEP)
+        project(0, 0, slot(0), "turn")
+        refill(0)
+        place(0, 0, STEP)
+        project(1, STEP, slot(1), "side")
+        project(0, STEP, slot(1), "turn")
+        refill(1)
+        project(1, 2 * STEP, slot(2), "turn")
+        place(1, STEP, RING)
+        project(0, 2 * STEP, slot(2), "turn")
+        refill(2)
+        for m in (0, 1):
+            project(m, RING, cover[:, STEP:], "turn")
+        place(0, STEP, LATE)
         for m in (1, 0):
-            project(m, 0)
-            place(m, 0, BANK)
+            project(m, LATE, first[:], "turn")
+            project(m, LATE + BANK, slot(2), "turn")
+        place(1, RING, S)
+        place(0, LATE, S)
         for m in (1, 0):
-            for s in range(BANK, S, BANK):
-                project(m, s)
-        place(1, BANK, S - LAST)
-        place(0, BANK, S)
-        place(1, S - LAST, S)
-        for m in range(2):
             nc.sync.dma_start(out[P * m : P * m + P, :], windows[m][:])

@@ -138,10 +138,10 @@ def tile_list_tabhs_gelu_kernel(tc, tab, w, b, wgo, offs, offs2, out):
         project(0, 0, slot(0), "turn")
         refill(0)
         place(0, 0, STEP)
-        project(1, STEP, slot(1), "side")
-        project(0, STEP, slot(1), "turn")
+        project(0, STEP, slot(1), "side0")
+        project(1, STEP, slot(1), "turn")
         refill(1)
-        project(1, 2 * STEP, slot(2), "turn")
+        project(1, 2 * STEP, slot(2), "side1")
         place(1, STEP, RING)
         project(0, 2 * STEP, slot(2), "turn")
         refill(2)

@@ -18,7 +18,7 @@ MULT = mybir.AluOpType.mult
 RING = 768
 BANK = 512
 STEP = 256
-LATE = S - RING
+LATE = S - 2 * STEP
 LIVE = 112
 SHARE = 1792
 LAST = 768
@@ -144,14 +144,13 @@ def tile_list_tabhs_gelu_kernel(tc, tab, w, b, wgo, offs, offs2, out):
         project(1, 2 * STEP, slot(2), "side1")
         place(1, STEP, RING)
         project(0, 2 * STEP, slot(2), "turn")
-        refill(2)
-        for m in (0, 1):
-            project(m, RING, cover[:, STEP:], "turn")
-        place(0, STEP, LATE)
+        project(0, RING, cover[:, STEP : STEP + BANK], "turn")
+        place(0, STEP, RING + BANK)
+        project(1, RING, cover[:, STEP : STEP + BANK], "turn")
         for m in (1, 0):
+            project(m, RING + BANK, cover[:, STEP + BANK :], "turn")
             project(m, LATE, first[:], "turn")
-            project(m, LATE + BANK, slot(2), "turn")
         place(1, RING, S)
-        place(0, LATE, S)
+        place(0, RING + BANK, S)
         for m in (1, 0):
             nc.sync.dma_start(out[P * m : P * m + P, :], windows[m][:])

@@ -15,37 +15,40 @@ COPY = mybir.ActivationFunctionType.Copy
 GELU = mybir.ActivationFunctionType.Gelu_apprx_tanh
 MULT = mybir.AluOpType.mult
 
-RING = 768
 BANK = 512
 STEP = 256
 LATE = S - 2 * STEP
 LIVE = 112
 SHARE = 1792
-LAST = 768
+HALF = 1024
 
 
 def tile_list_tabhs_gelu_kernel(tc, tab, w, b, wgo, offs, offs2, out):
     nc = tc.nc
     with (
         tc.tile_pool(name="keep", bufs=1) as keep,
+        tc.tile_pool(name="turns", bufs=1) as turns,
         tc.psum_pool(name="psum", bufs=1) as psum,
     ):
         idx = keep.tile([P, S // 16], U16, name="idx", align_bytes=256)
         idx2 = keep.tile([P, S // 16], U16, name="idx2", align_bytes=256)
         rows = keep.tile([P, T], U8, tag="rows", name="rows", align_bytes=256)
         words = keep.tile([P, T], I32, tag="wide", name="words", align_bytes=256)
-        w_raw = [keep.tile([P, 4, P], F32, tag="load%d" % m, name="w_raw%d" % m, align_bytes=256) for m in range(2)]
+        w_raw = [turns.tile([P, 4, P], F32, name="w_raw%d" % m, align_bytes=256, offset=1024 * m) for m in range(2)]
         bias = keep.tile([P, 2], F32, name="bias")
         window0 = keep.tile([P, T], F32, name="window0", align_bytes=256)
         window1 = keep.tile([P, T], F32, name="window1", align_bytes=256)
-        planes = [keep.tile([P, n], U8, name="plane%d" % n, align_bytes=256) for n in (RING, S - RING)]
+        planes = [keep.tile([P, n], U8, name="plane%d" % n, align_bytes=256) for n in (BANK, S - BANK)]
 
         scale_rows = tab[0, 512 * T : 528 * T].rearrange("(q t) -> q t", t=T)
         nc.sync.dma_start(rows[LIVE:P, :].bitcast(I32), scale_rows.bitcast(I32))
         nc.sync.dma_start(idx[:], offs)
         nc.sync.dma_start(words[:], tab[0, 0 : 512 * T].rearrange("(p c) -> p c", p=P).bitcast(I32))
-        for m in (1, 0):
+
+        def load_w(m):
             nc.sync.dma_start(w_raw[m][:], w[:, P * m : P * m + P].rearrange("(p j) n -> p j n", j=4))
+
+        load_w(1)
         with nc.allow_non_contiguous_dma(reason="256 values, one to a partition"):
             nc.sync.dma_start(bias[:], b.rearrange("(c p) -> p c", p=P))
         nc.sync.dma_start(idx2[:], offs2)
@@ -63,17 +66,17 @@ def tile_list_tabhs_gelu_kernel(tc, tab, w, b, wgo, offs, offs2, out):
         nc.vector.memset(warm[:, 0:1], 0.0)
         nc.scalar.activation(warm[:, 8:9], warm[:, 0:1], GELU)
 
-        picked = [keep.tile([P, n], U8, name="picked%d" % n, align_bytes=256) for n in (RING, S - RING)]
+        picked = [keep.tile([P, n], U8, name="picked%d" % n, align_bytes=256) for n in (BANK, S - BANK)]
 
         def move_scales(i):
             for r in range(4):
                 nc.sync.dma_start(planes[i][r:P:32, :].bitcast(I32), picked[i][LIVE + r : P : 4, :].bitcast(I32))
 
-        nc.vector.tensor_copy(picked[0][:], rows[:].indirect(idx[:, 0 : RING // 16]))
+        nc.vector.tensor_copy(picked[0][:], rows[:].indirect(idx[:, 0 : BANK // 16]))
         move_scales(0)
-        nc.vector.tensor_copy(picked[1][:], rows[:].indirect(idx[:, RING // 16 : S // 16]))
-        factor0 = keep.tile([P, STEP], F32, tag="rows", name="factor0", align_bytes=256)
-        nc.sync.dma_start(factor0[:], wgo[:, 0:STEP])
+        nc.vector.tensor_copy(picked[1][:], rows[:].indirect(idx[:, BANK // 16 : S // 16]))
+        factor0 = keep.tile([P, BANK], F32, tag="rows", name="factor0", align_bytes=256)
+        nc.sync.dma_start(factor0[:], wgo[:, 0:BANK])
         move_scales(1)
 
         group = [keep.tile([P, P, 4], BF16, tag="group%d" % m, name="group%d" % m, align_bytes=256) for m in range(2)]
@@ -97,60 +100,57 @@ def tile_list_tabhs_gelu_kernel(tc, tab, w, b, wgo, offs, offs2, out):
 
         first = keep.tile([P, BANK], U32, name="first", align_bytes=256)
         cast(1)
-        cast(0)
+        load_w(0)
         gather_words(first[:], 0, BANK)
         quantise(1)
-        cover = keep.tile([P, LATE - BANK], U32, tag="load1", name="cover", align_bytes=256)
+        cover = turns.tile([P, LATE - BANK], U32, name="cover", align_bytes=256, offset=2048)
         gather_words(cover[:], BANK, LATE)
-        quantise(0)
 
-        factor1 = keep.tile([P, S - STEP], F32, tag="group1", name="factor1", align_bytes=256)
-        nc.sync.dma_start(factor1[:], wgo[:, STEP:S])
+        factor1 = keep.tile([P, S - BANK], F32, tag="group1", name="factor1", align_bytes=256)
+        nc.sync.dma_start(factor1[:], wgo[:, BANK:S])
         windows = [window0, window1]
         y = [keep.tile([P, S], F32, name="y%d" % m, align_bytes=256) for m in range(2)]
 
-        def project(m, lo, codes, tag):
-            hi = lo + codes.shape[1]
-            bank = psum.tile([P, hi - lo], F32, tag=tag, name="bank%d_%d" % (m, lo))
-            nc.tensor.matmul_mx(
-                out=bank[:],
-                lhsT=w_codes[m][:].bitcast(FP8X4),
-                lhsT_scale=w_scales[m][:],
-                rhs=codes.bitcast(FP8X4),
-                rhs_scale=planes[0][:, lo:hi] if lo < RING else planes[1][:, lo - RING : hi - RING],
-                start=True,
-                stop=True,
-            )
-            nc.scalar.activation(y[m][:, lo:hi], bank[:], GELU, bias=bias[:, m : m + 1])
+        def project(m, lo, pieces, result):
+            hi = lo + sum(piece.shape[1] for piece in pieces)
+            bank = psum.tile([P, hi - lo], F32, tag="turn", name="bank%d_%d" % (m, lo))
+            at = lo
+            for piece in pieces:
+                end = at + piece.shape[1]
+                nc.tensor.matmul_mx(
+                    out=bank[:, at - lo : end - lo],
+                    lhsT=w_codes[m][:].bitcast(FP8X4),
+                    lhsT_scale=w_scales[m][:],
+                    rhs=piece.bitcast(FP8X4),
+                    rhs_scale=planes[0][:, at:end] if at < BANK else planes[1][:, at - BANK : end - BANK],
+                    start=True,
+                    stop=True,
+                )
+                at = end
+            nc.scalar.activation(result, bank[:], GELU, bias=bias[:, m : m + 1])
 
-        def place(m, lo, hi):
-            factor = factor0[:, lo:hi] if hi <= STEP else factor1[:, lo - STEP : hi - STEP]
-            nc.vector.tensor_tensor(windows[m][:].indirect(idx2[:, lo // 16 : hi // 16]), y[m][:, lo:hi], factor, MULT)
+        def place(m, lo, hi, result):
+            factor = factor0[:, lo:hi] if hi <= BANK else factor1[:, lo - BANK : hi - BANK]
+            nc.vector.tensor_tensor(windows[m][:].indirect(idx2[:, lo // 16 : hi // 16]), result, factor, MULT)
 
-        def slot(i):
-            return first[:, i * STEP : (i + 1) * STEP] if i < 2 else cover[:, 0:STEP]
-
-        def refill(i):
-            gather_words(slot(i), LATE + i * STEP, LATE + (i + 1) * STEP)
-
-        project(1, 0, slot(0), "turn")
-        place(1, 0, STEP)
-        project(0, 0, slot(0), "turn")
-        refill(0)
-        place(0, 0, STEP)
-        project(0, STEP, slot(1), "side0")
-        project(1, STEP, slot(1), "turn")
-        refill(1)
-        project(1, 2 * STEP, slot(2), "side1")
-        place(1, STEP, RING)
-        project(0, 2 * STEP, slot(2), "turn")
-        project(0, RING, cover[:, STEP : STEP + BANK], "turn")
-        place(0, STEP, RING + BANK)
-        project(1, RING, cover[:, STEP : STEP + BANK], "turn")
+        project(1, 0, [first[:, 0:STEP]], y[1][:, 0:STEP])
+        place(1, 0, STEP, y[1][:, 0:STEP])
+        cast(0)
+        quantise(0)
+        late = turns.tile([P, STEP], U32, name="late", align_bytes=256, offset=0)
+        gather_words(late[:], LATE, LATE + STEP)
+        second = turns.tile([P, STEP], F32, name="second", align_bytes=256, offset=1024)
+        project(1, STEP, [first[:, STEP:BANK]], second[:])
+        place(1, STEP, BANK, second[:])
+        project(0, 0, [first[:]], y[0][:, 0:BANK])
+        gather_words(first[:, 0:STEP], LATE + STEP, S)
+        place(0, 0, BANK, y[0][:, 0:BANK])
         for m in (1, 0):
-            project(m, RING + BANK, cover[:, STEP + BANK :], "turn")
-            project(m, LATE, first[:], "turn")
-        place(1, RING, S)
-        place(0, RING + BANK, S)
+            project(m, BANK, [cover[:, 0:BANK]], y[m][:, BANK:HALF])
+            place(m, BANK, HALF, y[m][:, BANK:HALF])
+        for m in (1, 0):
+            project(m, HALF, [cover[:, BANK:]], y[m][:, HALF:LATE])
+            project(m, LATE, [late[:], first[:, 0:STEP]], y[m][:, LATE:S])
+            place(m, HALF, S, y[m][:, HALF:S])
         for m in (1, 0):
             nc.sync.dma_start(out[P * m : P * m + P, :], windows[m][:])

@@ -17,7 +17,7 @@ MULT = mybir.AluOpType.mult
 
 BANK = 512
 STEP = 256
-LATE = S - 2 * STEP
+LATE = S - 3 * STEP
 LIVE = 112
 SHARE = 1792
 HALF = 1024
@@ -106,51 +106,63 @@ def tile_list_tabhs_gelu_kernel(tc, tab, w, b, wgo, offs, offs2, out):
         cover = turns.tile([P, LATE - BANK], U32, name="cover", align_bytes=256, offset=2048)
         gather_words(cover[:], BANK, LATE)
 
-        factor1 = keep.tile([P, S - BANK], F32, tag="group1", name="factor1", align_bytes=256)
-        nc.sync.dma_start(factor1[:], wgo[:, BANK:S])
+        factor1 = keep.tile([P, S - STEP], F32, tag="group1", name="factor1", align_bytes=256)
+        nc.sync.dma_start(factor1[:], wgo[:, STEP:S])
         windows = [window0, window1]
         y = [keep.tile([P, S], F32, name="y%d" % m, align_bytes=256) for m in range(2)]
 
-        def project(m, lo, pieces, result):
-            hi = lo + sum(piece.shape[1] for piece in pieces)
-            bank = psum.tile([P, hi - lo], F32, tag="turn", name="bank%d_%d" % (m, lo))
-            at = lo
-            for piece in pieces:
-                end = at + piece.shape[1]
-                nc.tensor.matmul_mx(
-                    out=bank[:, at - lo : end - lo],
-                    lhsT=w_codes[m][:].bitcast(FP8X4),
-                    lhsT_scale=w_scales[m][:],
-                    rhs=piece.bitcast(FP8X4),
-                    rhs_scale=planes[0][:, at:end] if at < BANK else planes[1][:, at - BANK : end - BANK],
-                    start=True,
-                    stop=True,
-                )
-                at = end
-            nc.scalar.activation(result, bank[:], GELU, bias=bias[:, m : m + 1])
+        def project(*jobs):
+            bank = psum.tile([P, BANK], F32, tag="turn", name="bank%d_%d" % jobs[0][0:2])
+            spans, at = [], 0
+            for m, lo, pieces, result in jobs:
+                start = at
+                for piece in pieces:
+                    n = piece.shape[1]
+                    nc.tensor.matmul_mx(
+                        out=bank[:, at : at + n],
+                        lhsT=w_codes[m][:].bitcast(FP8X4),
+                        lhsT_scale=w_scales[m][:],
+                        rhs=piece.bitcast(FP8X4),
+                        rhs_scale=planes[0][:, lo : lo + n] if lo < BANK else planes[1][:, lo - BANK : lo - BANK + n],
+                        start=True,
+                        stop=True,
+                    )
+                    at, lo = at + n, lo + n
+                spans.append((start, at))
+            for (m, lo, pieces, result), (start, end) in zip(jobs, spans):
+                nc.scalar.activation(result, bank[:, start:end], GELU, bias=bias[:, m : m + 1])
 
         def place(m, lo, hi, result):
-            factor = factor0[:, lo:hi] if hi <= BANK else factor1[:, lo - BANK : hi - BANK]
+            factor = factor0[:, lo:hi] if hi <= BANK else factor1[:, lo - STEP : hi - STEP]
             nc.vector.tensor_tensor(windows[m][:].indirect(idx2[:, lo // 16 : hi // 16]), result, factor, MULT)
 
-        project(1, 0, [first[:, 0:STEP]], y[1][:, 0:STEP])
+        def job(m, a, pieces):
+            lo = a * STEP
+            return m, lo, pieces, y[m][:, lo : lo + sum(piece.shape[1] for piece in pieces)]
+
+        project(job(1, 0, [first[:, 0:STEP]]))
         place(1, 0, STEP, y[1][:, 0:STEP])
         cast(0)
         quantise(0)
         late = turns.tile([P, STEP], U32, name="late", align_bytes=256, offset=0)
         gather_words(late[:], LATE, LATE + STEP)
         second = turns.tile([P, STEP], F32, name="second", align_bytes=256, offset=1024)
-        project(1, STEP, [first[:, STEP:BANK]], second[:])
+        project((1, STEP, [first[:, STEP:BANK]], second[:]))
         place(1, STEP, BANK, second[:])
-        project(0, 0, [first[:]], y[0][:, 0:BANK])
-        gather_words(first[:, 0:STEP], LATE + STEP, S)
-        place(0, 0, BANK, y[0][:, 0:BANK])
-        for m in (1, 0):
-            project(m, BANK, [cover[:, 0:BANK]], y[m][:, BANK:HALF])
-            place(m, BANK, HALF, y[m][:, BANK:HALF])
-        for m in (1, 0):
-            project(m, HALF, [cover[:, BANK:]], y[m][:, HALF:LATE])
-            project(m, LATE, [late[:], first[:, 0:STEP]], y[m][:, LATE:S])
-            place(m, HALF, S, y[m][:, HALF:S])
+        project(job(0, 0, [first[:, 0:STEP]]))
+        gather_words(first[:, 0:STEP], LATE + STEP, LATE + 2 * STEP)
+        place(0, 0, STEP, y[0][:, 0:STEP])
+        project(job(1, 2, [cover[:, 0:STEP]]), job(0, 1, [first[:, STEP:BANK]]))
+        gather_words(first[:, STEP:BANK], LATE + 2 * STEP, S)
+        place(1, BANK, 3 * STEP, y[1][:, BANK : 3 * STEP])
+        project(job(0, 2, [cover[:, 0:BANK]]))
+        place(0, STEP, HALF, y[0][:, STEP:HALF])
+        project(job(1, 3, [cover[:, STEP:]]))
+        project(job(1, 5, [late[:], first[:, 0:STEP]]))
+        project(job(1, 7, [first[:, STEP:BANK]]))
+        place(1, 3 * STEP, S, y[1][:, 3 * STEP : S])
+        project(job(0, 4, [cover[:, BANK:], late[:]]))
+        project(job(0, 6, [first[:]]))
+        place(0, HALF, S, y[0][:, HALF:S])
         for m in (1, 0):
             nc.sync.dma_start(out[P * m : P * m + P, :], windows[m][:])

@@ -107,7 +107,9 @@ def tile_list_tabhs_gelu_kernel(tc, tab, w, b, wgo, offs, offs2, out):
         gather_words(cover[:], BANK, LATE)
 
         factor1 = keep.tile([P, S - STEP], F32, tag="group1", name="factor1", align_bytes=256)
-        nc.sync.dma_start(factor1[:], wgo[:, STEP:S])
+        cuts = (STEP, BANK, 3 * STEP, HALF, HALF + BANK, S)
+        for lo, hi in zip(cuts, cuts[1:]):
+            nc.sync.dma_start(factor1[:, lo - STEP : hi - STEP], wgo[:, lo:hi])
         windows = [window0, window1]
         y = [keep.tile([P, S], F32, name="y%d" % m, align_bytes=256) for m in range(2)]
 

@@ -19,7 +19,7 @@ BANK = 512
 STEP = 256
 LATE = S - 3 * STEP
 LIVE = 112
-SHARE = 1792
+SHARE = 2048
 HALF = 1024
 
 
@@ -32,10 +32,11 @@ def tile_list_tabhs_gelu_kernel(tc, tab, w, b, wgo, offs, offs2, out):
     ):
         idx = keep.tile([P, S // 16], U16, name="idx", align_bytes=256)
         idx2 = keep.tile([P, S // 16], U16, name="idx2", align_bytes=256)
-        rows = keep.tile([P, T], U8, tag="rows", name="rows", align_bytes=256)
+        rows = turns.tile([P, T], U8, name="rows", align_bytes=256, offset=8192)
         words = keep.tile([P, T], I32, tag="wide", name="words", align_bytes=256)
-        w_raw = [turns.tile([P, 4, P], F32, name="w_raw%d" % m, align_bytes=256, offset=1024 * m) for m in range(2)]
-        bias = keep.tile([P, 2], F32, name="bias")
+        w_raw = [turns.tile([P, 4, P], F32, name="w_raw%d" % m, align_bytes=256, offset=at) for m, at in enumerate((7168, 1024))]
+        bias_first = turns.tile([P, 1], F32, name="bias_first", align_bytes=256, offset=16384)
+        bias = turns.tile([P, 2], F32, name="bias", align_bytes=256, offset=9216)
         window0 = keep.tile([P, T], F32, name="window0", align_bytes=256)
         window1 = keep.tile([P, T], F32, name="window1", align_bytes=256)
         planes = [keep.tile([P, n], U8, name="plane%d" % n, align_bytes=256) for n in (BANK, S - BANK)]
@@ -49,8 +50,8 @@ def tile_list_tabhs_gelu_kernel(tc, tab, w, b, wgo, offs, offs2, out):
             nc.sync.dma_start(w_raw[m][:], w[:, P * m : P * m + P].rearrange("(p j) n -> p j n", j=4))
 
         load_w(1)
-        with nc.allow_non_contiguous_dma(reason="256 values, one to a partition"):
-            nc.sync.dma_start(bias[:], b.rearrange("(c p) -> p c", p=P))
+        with nc.allow_non_contiguous_dma(reason="128 values, one to a partition"):
+            nc.sync.dma_start(bias_first[:], b[P:M].rearrange("(p c) -> p c", c=1))
         nc.sync.dma_start(idx2[:], offs2)
 
         def clear(ap, n, value):
@@ -59,12 +60,12 @@ def tile_list_tabhs_gelu_kernel(tc, tab, w, b, wgo, offs, offs2, out):
 
         nc.gpsimd.memset(rows[0:LIVE, :].bitcast(I32), 0)
         clear(window1[:], SHARE, 0.0)
-        nc.gpsimd.memset(window0[:], 0.0)
         nc.gpsimd.memset(window1[:, SHARE:T], 0.0)
 
         warm = keep.tile([P, 16], F32, name="warm")
-        nc.vector.memset(warm[:, 0:1], 0.0)
+        nc.gpsimd.memset(warm[:, 0:1], 0.0)
         nc.scalar.activation(warm[:, 8:9], warm[:, 0:1], GELU)
+        nc.gpsimd.memset(window0[:], 0.0)
 
         picked = [keep.tile([P, n], U8, name="picked%d" % n, align_bytes=256) for n in (BANK, S - BANK)]
 
@@ -75,11 +76,17 @@ def tile_list_tabhs_gelu_kernel(tc, tab, w, b, wgo, offs, offs2, out):
         nc.vector.tensor_copy(picked[0][:], rows[:].indirect(idx[:, 0 : BANK // 16]))
         move_scales(0)
         nc.vector.tensor_copy(picked[1][:], rows[:].indirect(idx[:, BANK // 16 : S // 16]))
-        factor0 = keep.tile([P, BANK], F32, tag="rows", name="factor0", align_bytes=256)
+        factor0 = turns.tile([P, BANK], F32, name="factor0", align_bytes=256, offset=10240)
         nc.sync.dma_start(factor0[:], wgo[:, 0:BANK])
+        load_w(0)
+        with nc.allow_non_contiguous_dma(reason="256 values, one to a partition"):
+            nc.sync.dma_start(bias[:], b.rearrange("(c p) -> p c", p=P))
         move_scales(1)
 
-        group = [keep.tile([P, P, 4], BF16, tag="group%d" % m, name="group%d" % m, align_bytes=256) for m in range(2)]
+        group = [
+            turns.tile([P, P, 4], BF16, name="group0", align_bytes=256, offset=16384),
+            keep.tile([P, P, 4], BF16, tag="group1", name="group1", align_bytes=256),
+        ]
         w_scales = [keep.tile([P, P], U8, name="w_scales%d" % m, align_bytes=256) for m in range(2)]
         w_codes = [keep.tile([P, P], U32, name="w_codes%d" % m, align_bytes=256) for m in range(2)]
 
@@ -100,14 +107,13 @@ def tile_list_tabhs_gelu_kernel(tc, tab, w, b, wgo, offs, offs2, out):
 
         first = keep.tile([P, BANK], U32, name="first", align_bytes=256)
         cast(1)
-        load_w(0)
         gather_words(first[:], 0, BANK)
         quantise(1)
         cover = turns.tile([P, LATE - BANK], U32, name="cover", align_bytes=256, offset=2048)
         gather_words(cover[:], BANK, LATE)
 
         factor1 = keep.tile([P, S - STEP], F32, tag="group1", name="factor1", align_bytes=256)
-        cuts = (STEP, BANK, 3 * STEP, HALF, HALF + BANK, S)
+        cuts = (STEP, 3 * STEP, HALF, HALF + BANK, S)
         for lo, hi in zip(cuts, cuts[1:]):
             nc.sync.dma_start(factor1[:, lo - STEP : hi - STEP], wgo[:, lo:hi])
         windows = [window0, window1]
@@ -132,7 +138,7 @@ def tile_list_tabhs_gelu_kernel(tc, tab, w, b, wgo, offs, offs2, out):
                     at, lo = at + n, lo + n
                 spans.append((start, at))
             for (m, lo, pieces, result), (start, end) in zip(jobs, spans):
-                nc.scalar.activation(result, bank[:, start:end], GELU, bias=bias[:, m : m + 1])
+                nc.scalar.activation(result, bank[:, start:end], GELU, bias=bias_first[:] if (m, lo) == (1, 0) else bias[:, m : m + 1])
 
         def place(m, lo, hi, result):
             factor = factor0[:, lo:hi] if hi <= BANK else factor1[:, lo - STEP : hi - STEP]
@@ -146,9 +152,9 @@ def tile_list_tabhs_gelu_kernel(tc, tab, w, b, wgo, offs, offs2, out):
         place(1, 0, STEP, y[1][:, 0:STEP])
         cast(0)
         quantise(0)
-        late = turns.tile([P, STEP], U32, name="late", align_bytes=256, offset=0)
+        late = turns.tile([P, STEP], U32, name="late", align_bytes=256, offset=7168)
         gather_words(late[:], LATE, LATE + STEP)
-        second = turns.tile([P, STEP], F32, name="second", align_bytes=256, offset=1024)
+        second = turns.tile([P, STEP], F32, name="second", align_bytes=256, offset=8192)
         project((1, STEP, [first[:, STEP:BANK]], second[:]))
         place(1, STEP, BANK, second[:])
         project(job(0, 0, [first[:, 0:STEP]]))

@@ -17,10 +17,10 @@ MULT = mybir.AluOpType.mult
 
 BANK = 512
 STEP = 256
-LATE = S - 3 * STEP
 LIVE = 112
 SHARE = 2048
 HALF = 1024
+FIRST = 384
 
 
 def tile_list_tabhs_gelu_kernel(tc, tab, w, b, wgo, offs, offs2, out):
@@ -33,23 +33,28 @@ def tile_list_tabhs_gelu_kernel(tc, tab, w, b, wgo, offs, offs2, out):
         idx = keep.tile([P, S // 16], U16, name="idx", align_bytes=256)
         idx2 = keep.tile([P, S // 16], U16, name="idx2", align_bytes=256)
         rows = turns.tile([P, T], U8, name="rows", align_bytes=256, offset=8192)
-        words = keep.tile([P, T], I32, tag="wide", name="words", align_bytes=256)
-        w_raw = [turns.tile([P, 4, P], F32, name="w_raw%d" % m, align_bytes=256, offset=at) for m, at in enumerate((7168, 1024))]
+        words = keep.tile([P, T], I32, name="words", align_bytes=256)
+        pair_early = keep.tile([P, 2, P], F32, name="pair_early", align_bytes=256)
+        carried = keep.tile([P // 2, 2, P], F32, name="carried", align_bytes=256)
+        pair_late = turns.tile([P, 2, P], F32, name="pair_late", align_bytes=256, offset=1024)
+        w_raw0 = turns.tile([P, 4, P], F32, name="w_raw0", align_bytes=256, offset=7168)
         bias_first = turns.tile([P, 1], F32, name="bias_first", align_bytes=256, offset=16384)
         bias = turns.tile([P, 2], F32, name="bias", align_bytes=256, offset=9216)
         window0 = keep.tile([P, T], F32, name="window0", align_bytes=256)
         window1 = keep.tile([P, T], F32, name="window1", align_bytes=256)
-        planes = [keep.tile([P, n], U8, name="plane%d" % n, align_bytes=256) for n in (BANK, S - BANK)]
+        planes = [
+            turns.tile([P, BANK], U8, name="plane_early", align_bytes=256, offset=20480),
+            keep.tile([P, S - BANK], U8, name="plane_late", align_bytes=256),
+        ]
 
         scale_rows = tab[0, 512 * T : 528 * T].rearrange("(q t) -> q t", t=T)
+        w1 = w[:, P:M].rearrange("(p j) n -> p j n", j=4)
         nc.sync.dma_start(rows[LIVE:P, :].bitcast(I32), scale_rows.bitcast(I32))
         nc.sync.dma_start(idx[:], offs)
+        nc.sync.dma_start(pair_early[0 : P // 2], w1[0 : P // 2, 2:4, :])
+        nc.sync.dma_start(carried[:], w1[P // 2 : P, 2:4, :])
         nc.sync.dma_start(words[:], tab[0, 0 : 512 * T].rearrange("(p c) -> p c", p=P).bitcast(I32))
-
-        def load_w(m):
-            nc.sync.dma_start(w_raw[m][:], w[:, P * m : P * m + P].rearrange("(p j) n -> p j n", j=4))
-
-        load_w(1)
+        nc.sync.dma_start(pair_late[:], w1[:, 0:2, :])
         with nc.allow_non_contiguous_dma(reason="128 values, one to a partition"):
             nc.sync.dma_start(bias_first[:], b[P:M].rearrange("(p c) -> p c", c=1))
         nc.sync.dma_start(idx2[:], offs2)
@@ -76,11 +81,13 @@ def tile_list_tabhs_gelu_kernel(tc, tab, w, b, wgo, offs, offs2, out):
         nc.vector.tensor_copy(picked[0][:], rows[:].indirect(idx[:, 0 : BANK // 16]))
         move_scales(0)
         nc.vector.tensor_copy(picked[1][:], rows[:].indirect(idx[:, BANK // 16 : S // 16]))
-        factor0 = turns.tile([P, BANK], F32, name="factor0", align_bytes=256, offset=10240)
-        nc.sync.dma_start(factor0[:], wgo[:, 0:BANK])
-        load_w(0)
+        factor0 = turns.tile([P, STEP], F32, name="factor0", align_bytes=256, offset=10240)
+        nc.sync.dma_start(factor0[:], wgo[:, 0:STEP])
+        nc.sync.dma_start(w_raw0[:], w[:, 0:P].rearrange("(p j) n -> p j n", j=4))
         with nc.allow_non_contiguous_dma(reason="256 values, one to a partition"):
             nc.sync.dma_start(bias[:], b.rearrange("(c p) -> p c", p=P))
+        factor1 = turns.tile([P, BANK], F32, name="factor1", align_bytes=256, offset=11264)
+        nc.sync.dma_start(factor1[:], wgo[:, STEP : 3 * STEP])
         move_scales(1)
 
         group = [
@@ -90,10 +97,8 @@ def tile_list_tabhs_gelu_kernel(tc, tab, w, b, wgo, offs, offs2, out):
         w_scales = [keep.tile([P, P], U8, name="w_scales%d" % m, align_bytes=256) for m in range(2)]
         w_codes = [keep.tile([P, P], U32, name="w_codes%d" % m, align_bytes=256) for m in range(2)]
 
-        def cast(m):
-            cast_out = group[m][:].rearrange("p (c i) j -> p c j i", i=4)
-            cast_in = w_raw[m][:].rearrange("p j (c i) -> p c j i", i=4)
-            nc.scalar.activation(cast_out, cast_in, COPY)
+        def cast(dst, src):
+            nc.scalar.activation(dst.rearrange("p (c i) j -> p c j i", i=4), src.rearrange("p j (c i) -> p c j i", i=4), COPY)
 
         def quantise(m):
             nc.vector.quantize_mx(
@@ -105,22 +110,22 @@ def tile_list_tabhs_gelu_kernel(tc, tab, w, b, wgo, offs, offs2, out):
         def gather_words(dst, lo, hi):
             nc.vector.tensor_copy(dst, words[:].bitcast(U32).indirect(idx[:, lo // 16 : hi // 16]))
 
-        first = keep.tile([P, BANK], U32, name="first", align_bytes=256)
-        cast(1)
-        gather_words(first[:], 0, BANK)
+        nc.scalar.copy(pair_early[P // 2 : P].rearrange("p j n -> p (j n)"), carried[:].rearrange("p j n -> p (j n)"))
+        cast(group[1][:, :, 2:4], pair_early[:])
+        first = keep.tile([P, FIRST], U32, name="first", align_bytes=256)
+        cast(group[1][:, :, 0:2], pair_late[:])
+        gather_words(first[:], 0, FIRST)
         quantise(1)
-        cover = turns.tile([P, LATE - BANK], U32, name="cover", align_bytes=256, offset=2048)
-        gather_words(cover[:], BANK, LATE)
+        cover = turns.tile([P, HALF - FIRST], U32, name="cover", align_bytes=256, offset=1024)
+        gather_words(cover[:], FIRST, HALF)
 
-        factor1 = keep.tile([P, S - STEP], F32, tag="group1", name="factor1", align_bytes=256)
-        cuts = (STEP, 3 * STEP, HALF, HALF + BANK, S)
-        for lo, hi in zip(cuts, cuts[1:]):
-            nc.sync.dma_start(factor1[:, lo - STEP : hi - STEP], wgo[:, lo:hi])
+        factor2 = keep.tile([P, S - 3 * STEP], F32, tag="group1", name="factor2", align_bytes=256)
+        nc.sync.dma_start(factor2[:], wgo[:, 3 * STEP : S])
         windows = [window0, window1]
         y = [keep.tile([P, S], F32, name="y%d" % m, align_bytes=256) for m in range(2)]
 
-        def project(*jobs):
-            bank = psum.tile([P, BANK], F32, tag="turn", name="bank%d_%d" % jobs[0][0:2])
+        def project(tag, *jobs):
+            bank = psum.tile([P, BANK], F32, tag=tag, name="bank%d_%d" % jobs[0][0:2])
             spans, at = [], 0
             for m, lo, pieces, result in jobs:
                 start = at
@@ -138,39 +143,45 @@ def tile_list_tabhs_gelu_kernel(tc, tab, w, b, wgo, offs, offs2, out):
                     at, lo = at + n, lo + n
                 spans.append((start, at))
             for (m, lo, pieces, result), (start, end) in zip(jobs, spans):
-                nc.scalar.activation(result, bank[:, start:end], GELU, bias=bias_first[:] if (m, lo) == (1, 0) else bias[:, m : m + 1])
+                nc.scalar.activation(result, bank[:, start:end], GELU, bias=bias_first[:] if m == 1 and lo < STEP else bias[:, m : m + 1])
 
         def place(m, lo, hi, result):
-            factor = factor0[:, lo:hi] if hi <= BANK else factor1[:, lo - STEP : hi - STEP]
+            share, base = (factor0, 0) if hi <= STEP else (factor1, STEP) if hi <= 3 * STEP else (factor2, 3 * STEP)
+            factor = share[:, lo - base : hi - base]
             nc.vector.tensor_tensor(windows[m][:].indirect(idx2[:, lo // 16 : hi // 16]), result, factor, MULT)
 
-        def job(m, a, pieces):
-            lo = a * STEP
+        def job(m, lo, pieces):
             return m, lo, pieces, y[m][:, lo : lo + sum(piece.shape[1] for piece in pieces)]
 
-        project(job(1, 0, [first[:, 0:STEP]]))
+        at = BANK - FIRST
+        across = [first[:, STEP:FIRST], cover[:, 0:at]]
+        project("early", job(1, 0, [first[:, 0:P]]))
+        project("turn", job(1, P, [first[:, P:STEP]]))
         place(1, 0, STEP, y[1][:, 0:STEP])
-        cast(0)
+        cast(group[0][:], w_raw0[:])
         quantise(0)
         late = turns.tile([P, STEP], U32, name="late", align_bytes=256, offset=7168)
-        gather_words(late[:], LATE, LATE + STEP)
+        gather_words(late[:], 4 * STEP, 5 * STEP)
         second = turns.tile([P, STEP], F32, name="second", align_bytes=256, offset=8192)
-        project((1, STEP, [first[:, STEP:BANK]], second[:]))
+        project("turn", (1, STEP, across, second[:]))
         place(1, STEP, BANK, second[:])
-        project(job(0, 0, [first[:, 0:STEP]]))
-        gather_words(first[:, 0:STEP], LATE + STEP, LATE + 2 * STEP)
+        project("turn", job(0, 0, [first[:, 0:STEP]]))
+        gather_words(first[:, 0:STEP], 5 * STEP, 6 * STEP)
         place(0, 0, STEP, y[0][:, 0:STEP])
-        project(job(1, 2, [cover[:, 0:STEP]]), job(0, 1, [first[:, STEP:BANK]]))
-        gather_words(first[:, STEP:BANK], LATE + 2 * STEP, S)
+        project("turn", job(1, BANK, [cover[:, at : at + STEP]]), job(0, STEP, across))
+        later = turns.tile([P, STEP], U32, name="later", align_bytes=256, offset=20480)
+        gather_words(later[:], 6 * STEP, 7 * STEP)
         place(1, BANK, 3 * STEP, y[1][:, BANK : 3 * STEP])
-        project(job(0, 2, [cover[:, 0:BANK]]))
-        place(0, STEP, HALF, y[0][:, STEP:HALF])
-        project(job(1, 3, [cover[:, STEP:]]))
-        project(job(1, 5, [late[:], first[:, 0:STEP]]))
-        project(job(1, 7, [first[:, STEP:BANK]]))
+        project("turn", job(0, BANK, [cover[:, at : at + STEP]]))
+        gather_words(cover[:, at : at + STEP], 7 * STEP, S)
+        place(0, STEP, 3 * STEP, y[0][:, STEP : 3 * STEP])
+        project("turn", job(1, 3 * STEP, [cover[:, at + STEP :], late[:]]))
+        project("turn", job(1, 5 * STEP, [first[:, 0:STEP], later[:]]))
+        project("turn", job(1, 7 * STEP, [cover[:, at : at + STEP]]))
         place(1, 3 * STEP, S, y[1][:, 3 * STEP : S])
-        project(job(0, 4, [cover[:, BANK:], late[:]]))
-        project(job(0, 6, [first[:]]))
-        place(0, HALF, S, y[0][:, HALF:S])
+        project("turn", job(0, 3 * STEP, [cover[:, at + STEP :], late[:]]))
+        project("turn", job(0, 5 * STEP, [first[:, 0:STEP], later[:]]))
+        project("turn", job(0, 7 * STEP, [cover[:, at : at + STEP]]))
+        place(0, 3 * STEP, S, y[0][:, 3 * STEP : S])
         for m in (1, 0):
             nc.sync.dma_start(out[P * m : P * m + P, :], windows[m][:])

@@ -18,7 +18,7 @@ MULT = mybir.AluOpType.mult
 BANK = 512
 STEP = 256
 LIVE = 112
-SHARE = 2048
+SHARE = 1792
 HALF = 1024
 FIRST = 384
 

@@ -18,9 +18,8 @@ MULT = mybir.AluOpType.mult
 BANK = 512
 STEP = 256
 LIVE = 112
-SHARE = 1792
-HALF = 1024
-FIRST = 384
+SHARE = 2048
+EARLY = 640
 
 
 def tile_list_tabhs_gelu_kernel(tc, tab, w, b, wgo, offs, offs2, out):
@@ -32,68 +31,40 @@ def tile_list_tabhs_gelu_kernel(tc, tab, w, b, wgo, offs, offs2, out):
     ):
         idx = keep.tile([P, S // 16], U16, name="idx", align_bytes=256)
         idx2 = keep.tile([P, S // 16], U16, name="idx2", align_bytes=256)
-        rows = turns.tile([P, T], U8, name="rows", align_bytes=256, offset=8192)
         words = keep.tile([P, T], I32, name="words", align_bytes=256)
-        pair_early = keep.tile([P, 2, P], F32, name="pair_early", align_bytes=256)
         carried = keep.tile([P // 2, 2, P], F32, name="carried", align_bytes=256)
-        pair_late = turns.tile([P, 2, P], F32, name="pair_late", align_bytes=256, offset=1024)
-        w_raw0 = turns.tile([P, 4, P], F32, name="w_raw0", align_bytes=256, offset=7168)
-        bias_first = turns.tile([P, 1], F32, name="bias_first", align_bytes=256, offset=16384)
-        bias = turns.tile([P, 2], F32, name="bias", align_bytes=256, offset=9216)
-        window0 = keep.tile([P, T], F32, name="window0", align_bytes=256)
+        w_raw0 = keep.tile([P, 4, P], F32, name="w_raw0", align_bytes=256)
         window1 = keep.tile([P, T], F32, name="window1", align_bytes=256)
-        planes = [
-            turns.tile([P, BANK], U8, name="plane_early", align_bytes=256, offset=20480),
-            keep.tile([P, S - BANK], U8, name="plane_late", align_bytes=256),
-        ]
+        w_raw1 = turns.tile([P, 4, P], F32, name="w_raw1", align_bytes=256, offset=1024)
+        group1 = turns.tile([P, P, 4], BF16, name="group1", align_bytes=256, offset=5376)
+        rows = turns.tile([P, T], U8, name="rows", align_bytes=256, offset=22528)
+        bias1 = keep.tile([P, 1], F32, name="bias1", align_bytes=256)
 
         scale_rows = tab[0, 512 * T : 528 * T].rearrange("(q t) -> q t", t=T)
         w1 = w[:, P:M].rearrange("(p j) n -> p j n", j=4)
         nc.sync.dma_start(rows[LIVE:P, :].bitcast(I32), scale_rows.bitcast(I32))
         nc.sync.dma_start(idx[:], offs)
-        nc.sync.dma_start(pair_early[0 : P // 2], w1[0 : P // 2, 2:4, :])
         nc.sync.dma_start(carried[:], w1[P // 2 : P, 2:4, :])
-        nc.sync.dma_start(words[:], tab[0, 0 : 512 * T].rearrange("(p c) -> p c", p=P).bitcast(I32))
-        nc.sync.dma_start(pair_late[:], w1[:, 0:2, :])
-        with nc.allow_non_contiguous_dma(reason="128 values, one to a partition"):
-            nc.sync.dma_start(bias_first[:], b[P:M].rearrange("(p c) -> p c", c=1))
+        nc.sync.dma_start(w_raw1[0 : P // 2, 2:4, :], w1[0 : P // 2, 2:4, :])
+        nc.sync.dma_start(w_raw1[:, 0:2, :], w1[:, 0:2, :])
         nc.sync.dma_start(idx2[:], offs2)
+        nc.sync.dma_start(words[:], tab[0, 0 : 512 * T].rearrange("(p c) -> p c", p=P).bitcast(I32))
+        nc.sync.dma_start(w_raw0[:], w[:, 0:P].rearrange("(p j) n -> p j n", j=4))
+        with nc.allow_non_contiguous_dma(reason="128 values, one to a partition"):
+            nc.sync.dma_start(bias1[:], b[P:M].rearrange("(p c) -> p c", c=1))
 
         def clear(ap, n, value):
             nc.vector.memset(ap[:, 0 : n // 2 - 1], value)
             nc.vector.memset(ap[:, n // 2 - 1 : n], value)
 
         nc.gpsimd.memset(rows[0:LIVE, :].bitcast(I32), 0)
-        clear(window1[:], SHARE, 0.0)
-        nc.gpsimd.memset(window1[:, SHARE:T], 0.0)
-
         warm = keep.tile([P, 16], F32, name="warm")
         nc.gpsimd.memset(warm[:, 0:1], 0.0)
         nc.scalar.activation(warm[:, 8:9], warm[:, 0:1], GELU)
-        nc.gpsimd.memset(window0[:], 0.0)
+        clear(window1[:], SHARE, 0.0)
+        nc.gpsimd.memset(window1[:, SHARE:T], 0.0)
 
-        picked = [keep.tile([P, n], U8, name="picked%d" % n, align_bytes=256) for n in (BANK, S - BANK)]
-
-        def move_scales(i):
-            for r in range(4):
-                nc.sync.dma_start(planes[i][r:P:32, :].bitcast(I32), picked[i][LIVE + r : P : 4, :].bitcast(I32))
-
-        nc.vector.tensor_copy(picked[0][:], rows[:].indirect(idx[:, 0 : BANK // 16]))
-        move_scales(0)
-        nc.vector.tensor_copy(picked[1][:], rows[:].indirect(idx[:, BANK // 16 : S // 16]))
-        factor0 = turns.tile([P, STEP], F32, name="factor0", align_bytes=256, offset=10240)
-        nc.sync.dma_start(factor0[:], wgo[:, 0:STEP])
-        nc.sync.dma_start(w_raw0[:], w[:, 0:P].rearrange("(p j) n -> p j n", j=4))
-        with nc.allow_non_contiguous_dma(reason="256 values, one to a partition"):
-            nc.sync.dma_start(bias[:], b.rearrange("(c p) -> p c", p=P))
-        factor1 = turns.tile([P, BANK], F32, name="factor1", align_bytes=256, offset=11264)
-        nc.sync.dma_start(factor1[:], wgo[:, STEP : 3 * STEP])
-        move_scales(1)
-
-        group = [
-            turns.tile([P, P, 4], BF16, name="group0", align_bytes=256, offset=16384),
-            keep.tile([P, P, 4], BF16, tag="group1", name="group1", align_bytes=256),
-        ]
+        group = [keep.tile([P, P, 4], BF16, name="group0", align_bytes=256), group1]
         w_scales = [keep.tile([P, P], U8, name="w_scales%d" % m, align_bytes=256) for m in range(2)]
         w_codes = [keep.tile([P, P], U32, name="w_codes%d" % m, align_bytes=256) for m in range(2)]
 
@@ -107,81 +78,99 @@ def tile_list_tabhs_gelu_kernel(tc, tab, w, b, wgo, offs, offs2, out):
                 in_=group[m][:].rearrange("p n j -> p (n j)"),
             )
 
+        picked_early = keep.tile([P, EARLY], U8, name="picked_early", align_bytes=256)
+        nc.vector.tensor_copy(picked_early[:], rows[:].indirect(idx[:, 0 : EARLY // 16]))
+        nc.scalar.copy(w_raw1[P // 2 : P, 2:4, :].rearrange("p j n -> p (j n)"), carried[:].rearrange("p j n -> p (j n)"))
+        cast(group1[:], w_raw1[:])
+        plane = turns.tile([P, S], U8, name="plane", align_bytes=256, offset=0)
+        picked_late = turns.tile([P, S - EARLY], U8, name="picked_late", align_bytes=256, offset=2048)
+
+        def move_scales(queue, picked, lo, hi):
+            for r in range(4):
+                queue.dma_start(plane[r:P:32, lo:hi].bitcast(I32), picked[LIVE + r : P : 4, :].bitcast(I32))
+
+        move_scales(nc.scalar, picked_early, 0, EARLY)
+        quantise(1)
+        factor0 = turns.tile([P, STEP], F32, name="factor0", align_bytes=256, offset=4608)
+        nc.sync.dma_start(factor0[:], wgo[:, 0:STEP])
+        window0 = turns.tile([P, T], F32, name="window0", align_bytes=256, offset=6144)
+        nc.gpsimd.memset(window0[:], 0.0)
+        nc.vector.tensor_copy(picked_late[:], rows[:].indirect(idx[:, EARLY // 16 : S // 16]))
+
+        bias0 = turns.tile([P, 1], F32, name="bias0", align_bytes=256, offset=22528)
+        with nc.allow_non_contiguous_dma(reason="128 values, one to a partition"):
+            nc.sync.dma_start(bias0[:], b[0:P].rearrange("(p c) -> p c", c=1))
+        move_scales(nc.sync, picked_late, EARLY, S)
+        factor1 = turns.tile([P, S - STEP], F32, name="factor1", align_bytes=256, offset=22784)
+        nc.sync.dma_start(factor1[:, 0 : 3 * STEP], wgo[:, STEP : 4 * STEP])
+        nc.sync.dma_start(factor1[:, 3 * STEP :], wgo[:, 4 * STEP : S])
+        bias = [bias0, bias1]
+
         def gather_words(dst, lo, hi):
             nc.vector.tensor_copy(dst, words[:].bitcast(U32).indirect(idx[:, lo // 16 : hi // 16]))
 
-        nc.scalar.copy(pair_early[P // 2 : P].rearrange("p j n -> p (j n)"), carried[:].rearrange("p j n -> p (j n)"))
-        cast(group[1][:, :, 2:4], pair_early[:])
-        first = keep.tile([P, FIRST], U32, name="first", align_bytes=256)
-        cast(group[1][:, :, 0:2], pair_late[:])
-        gather_words(first[:], 0, FIRST)
-        quantise(1)
-        cover = turns.tile([P, HALF - FIRST], U32, name="cover", align_bytes=256, offset=1024)
-        gather_words(cover[:], FIRST, HALF)
+        first = keep.tile([P, STEP], U32, name="first", align_bytes=256)
+        cover = keep.tile([P, BANK], U32, name="cover", align_bytes=256)
+        gather_words(first[:], 0, STEP)
+        gather_words(cover[:], STEP, 3 * STEP)
+        cast(group[0][:], w_raw0[:])
+        quantise(0)
 
-        factor2 = keep.tile([P, S - 3 * STEP], F32, tag="group1", name="factor2", align_bytes=256)
-        nc.sync.dma_start(factor2[:], wgo[:, 3 * STEP : S])
         windows = [window0, window1]
         y = [keep.tile([P, S], F32, name="y%d" % m, align_bytes=256) for m in range(2)]
+
+        slots = [first[:], cover[:, 0:STEP], cover[:, STEP:BANK]]
 
         def project(tag, *jobs):
             bank = psum.tile([P, BANK], F32, tag=tag, name="bank%d_%d" % jobs[0][0:2])
             spans, at = [], 0
-            for m, lo, pieces, result in jobs:
-                start = at
-                for piece in pieces:
-                    n = piece.shape[1]
+            for m, lo, hi in jobs:
+                spans.append((at, at + hi - lo))
+                for start in range(lo, hi, STEP):
+                    n = min(STEP, hi - start)
                     nc.tensor.matmul_mx(
                         out=bank[:, at : at + n],
                         lhsT=w_codes[m][:].bitcast(FP8X4),
                         lhsT_scale=w_scales[m][:],
-                        rhs=piece.bitcast(FP8X4),
-                        rhs_scale=planes[0][:, lo : lo + n] if lo < BANK else planes[1][:, lo - BANK : lo - BANK + n],
+                        rhs=slots[start // STEP % 3][:, start % STEP : start % STEP + n].bitcast(FP8X4),
+                        rhs_scale=plane[:, start : start + n],
                         start=True,
                         stop=True,
                     )
-                    at, lo = at + n, lo + n
-                spans.append((start, at))
-            for (m, lo, pieces, result), (start, end) in zip(jobs, spans):
-                nc.scalar.activation(result, bank[:, start:end], GELU, bias=bias_first[:] if m == 1 and lo < STEP else bias[:, m : m + 1])
+                    at = at + n
+            for (m, lo, hi), (start, end) in reversed(list(zip(jobs, spans))):
+                nc.scalar.activation(y[m][:, lo:hi], bank[:, start:end], GELU, bias=bias[m][:])
 
-        def place(m, lo, hi, result):
-            share, base = (factor0, 0) if hi <= STEP else (factor1, STEP) if hi <= 3 * STEP else (factor2, 3 * STEP)
-            factor = share[:, lo - base : hi - base]
-            nc.vector.tensor_tensor(windows[m][:].indirect(idx2[:, lo // 16 : hi // 16]), result, factor, MULT)
+        def place(m, lo, hi):
+            factor = factor0[:] if hi == STEP else factor1[:, lo - STEP : hi - STEP]
+            nc.vector.tensor_tensor(windows[m][:].indirect(idx2[:, lo // 16 : hi // 16]), y[m][:, lo:hi], factor, MULT)
 
-        def job(m, lo, pieces):
-            return m, lo, pieces, y[m][:, lo : lo + sum(piece.shape[1] for piece in pieces)]
+        def gather_block(block):
+            gather_words(slots[block % 3], block * STEP, (block + 1) * STEP)
 
-        at = BANK - FIRST
-        across = [first[:, STEP:FIRST], cover[:, 0:at]]
-        project("early", job(1, 0, [first[:, 0:P]]))
-        project("turn", job(1, P, [first[:, P:STEP]]))
-        place(1, 0, STEP, y[1][:, 0:STEP])
-        cast(group[0][:], w_raw0[:])
-        quantise(0)
-        late = turns.tile([P, STEP], U32, name="late", align_bytes=256, offset=7168)
-        gather_words(late[:], 4 * STEP, 5 * STEP)
-        second = turns.tile([P, STEP], F32, name="second", align_bytes=256, offset=8192)
-        project("turn", (1, STEP, across, second[:]))
-        place(1, STEP, BANK, second[:])
-        project("turn", job(0, 0, [first[:, 0:STEP]]))
-        gather_words(first[:, 0:STEP], 5 * STEP, 6 * STEP)
-        place(0, 0, STEP, y[0][:, 0:STEP])
-        project("turn", job(1, BANK, [cover[:, at : at + STEP]]), job(0, STEP, across))
-        later = turns.tile([P, STEP], U32, name="later", align_bytes=256, offset=20480)
-        gather_words(later[:], 6 * STEP, 7 * STEP)
-        place(1, BANK, 3 * STEP, y[1][:, BANK : 3 * STEP])
-        project("turn", job(0, BANK, [cover[:, at : at + STEP]]))
-        gather_words(cover[:, at : at + STEP], 7 * STEP, S)
-        place(0, STEP, 3 * STEP, y[0][:, STEP : 3 * STEP])
-        project("turn", job(1, 3 * STEP, [cover[:, at + STEP :], late[:]]))
-        project("turn", job(1, 5 * STEP, [first[:, 0:STEP], later[:]]))
-        project("turn", job(1, 7 * STEP, [cover[:, at : at + STEP]]))
-        place(1, 3 * STEP, S, y[1][:, 3 * STEP : S])
-        project("turn", job(0, 3 * STEP, [cover[:, at + STEP :], late[:]]))
-        project("turn", job(0, 5 * STEP, [first[:, 0:STEP], later[:]]))
-        project("turn", job(0, 7 * STEP, [cover[:, at : at + STEP]]))
-        place(0, 3 * STEP, S, y[0][:, 3 * STEP : S])
+        project("a", (1, 0, P))
+        project("b", (1, P, STEP))
+        place(1, 0, STEP)
+        project("a", (1, STEP, 2 * STEP))
+        project("b", (0, 0, STEP))
+        gather_block(3)
+        place(0, 0, STEP)
+        project("b", (0, STEP, 2 * STEP), (1, 2 * STEP, 3 * STEP))
+        gather_block(4)
+        place(1, STEP, 3 * STEP)
+        project("b", (0, 2 * STEP, 4 * STEP))
+        gather_block(5)
+        place(0, STEP, 4 * STEP)
+        project("b", (1, 3 * STEP, 5 * STEP))
+        gather_block(6)
+        place(1, 3 * STEP, 5 * STEP)
+        project("b", (0, 4 * STEP, 6 * STEP))
+        gather_block(7)
+        place(0, 4 * STEP, 5 * STEP)
+        project("b", (1, 5 * STEP, 7 * STEP))
+        project("b", (1, 7 * STEP, S))
+        place(1, 5 * STEP, S)
+        project("b", (0, 6 * STEP, S))
+        place(0, 5 * STEP, S)
         for m in (1, 0):
             nc.sync.dma_start(out[P * m : P * m + P, :], windows[m][:])

@@ -19,7 +19,7 @@ BANK = 512
 STEP = 256
 LIVE = 112
 SHARE = 2048
-EARLY = 640
+EARLY = 576
 
 
 def tile_list_tabhs_gelu_kernel(tc, tab, w, b, wgo, offs, offs2, out):
@@ -33,12 +33,10 @@ def tile_list_tabhs_gelu_kernel(tc, tab, w, b, wgo, offs, offs2, out):
         idx2 = keep.tile([P, S // 16], U16, name="idx2", align_bytes=256)
         words = keep.tile([P, T], I32, name="words", align_bytes=256)
         carried = keep.tile([P // 2, 2, P], F32, name="carried", align_bytes=256)
-        w_raw0 = keep.tile([P, 4, P], F32, name="w_raw0", align_bytes=256)
         window1 = keep.tile([P, T], F32, name="window1", align_bytes=256)
         w_raw1 = turns.tile([P, 4, P], F32, name="w_raw1", align_bytes=256, offset=1024)
         group1 = turns.tile([P, P, 4], BF16, name="group1", align_bytes=256, offset=5376)
         rows = turns.tile([P, T], U8, name="rows", align_bytes=256, offset=22528)
-        bias1 = keep.tile([P, 1], F32, name="bias1", align_bytes=256)
 
         scale_rows = tab[0, 512 * T : 528 * T].rearrange("(q t) -> q t", t=T)
         w1 = w[:, P:M].rearrange("(p j) n -> p j n", j=4)
@@ -47,11 +45,8 @@ def tile_list_tabhs_gelu_kernel(tc, tab, w, b, wgo, offs, offs2, out):
         nc.sync.dma_start(carried[:], w1[P // 2 : P, 2:4, :])
         nc.sync.dma_start(w_raw1[0 : P // 2, 2:4, :], w1[0 : P // 2, 2:4, :])
         nc.sync.dma_start(w_raw1[:, 0:2, :], w1[:, 0:2, :])
-        nc.sync.dma_start(idx2[:], offs2)
         nc.sync.dma_start(words[:], tab[0, 0 : 512 * T].rearrange("(p c) -> p c", p=P).bitcast(I32))
-        nc.sync.dma_start(w_raw0[:], w[:, 0:P].rearrange("(p j) n -> p j n", j=4))
-        with nc.allow_non_contiguous_dma(reason="128 values, one to a partition"):
-            nc.sync.dma_start(bias1[:], b[P:M].rearrange("(p c) -> p c", c=1))
+        nc.sync.dma_start(idx2[:], offs2)
 
         def clear(ap, n, value):
             nc.vector.memset(ap[:, 0 : n // 2 - 1], value)
@@ -82,14 +77,19 @@ def tile_list_tabhs_gelu_kernel(tc, tab, w, b, wgo, offs, offs2, out):
         nc.vector.tensor_copy(picked_early[:], rows[:].indirect(idx[:, 0 : EARLY // 16]))
         nc.scalar.copy(w_raw1[P // 2 : P, 2:4, :].rearrange("p j n -> p (j n)"), carried[:].rearrange("p j n -> p (j n)"))
         cast(group1[:], w_raw1[:])
-        plane = turns.tile([P, S], U8, name="plane", align_bytes=256, offset=0)
-        picked_late = turns.tile([P, S - EARLY], U8, name="picked_late", align_bytes=256, offset=2048)
+        plane = keep.tile([P, S], U8, name="plane", align_bytes=256)
+        picked_late = turns.tile([P, S - EARLY], U8, name="picked_late", align_bytes=256, offset=2304)
 
-        def move_scales(queue, picked, lo, hi):
+        def move_scales(picked, lo, hi):
             for r in range(4):
-                queue.dma_start(plane[r:P:32, lo:hi].bitcast(I32), picked[LIVE + r : P : 4, :].bitcast(I32))
+                nc.sync.dma_start(plane[r:P:32, lo:hi].bitcast(I32), picked[LIVE + r : P : 4, :].bitcast(I32))
 
-        move_scales(nc.scalar, picked_early, 0, EARLY)
+        move_scales(picked_early, 0, EARLY)
+        w_raw0 = turns.tile([P, 4, P], F32, name="w_raw0", align_bytes=256, offset=0)
+        nc.sync.dma_start(w_raw0[:], w[:, 0:P].rearrange("(p j) n -> p j n", j=4))
+        bias1 = turns.tile([P, 1], F32, name="bias1", align_bytes=256, offset=2048)
+        with nc.allow_non_contiguous_dma(reason="128 values, one to a partition"):
+            nc.sync.dma_start(bias1[:], b[P:M].rearrange("(p c) -> p c", c=1))
         quantise(1)
         factor0 = turns.tile([P, STEP], F32, name="factor0", align_bytes=256, offset=4608)
         nc.sync.dma_start(factor0[:], wgo[:, 0:STEP])
@@ -100,7 +100,7 @@ def tile_list_tabhs_gelu_kernel(tc, tab, w, b, wgo, offs, offs2, out):
         bias0 = turns.tile([P, 1], F32, name="bias0", align_bytes=256, offset=22528)
         with nc.allow_non_contiguous_dma(reason="128 values, one to a partition"):
             nc.sync.dma_start(bias0[:], b[0:P].rearrange("(p c) -> p c", c=1))
-        move_scales(nc.sync, picked_late, EARLY, S)
+        move_scales(picked_late, EARLY, S)
         factor1 = turns.tile([P, S - STEP], F32, name="factor1", align_bytes=256, offset=22784)
         nc.sync.dma_start(factor1[:, 0 : 3 * STEP], wgo[:, STEP : 4 * STEP])
         nc.sync.dma_start(factor1[:, 3 * STEP :], wgo[:, 4 * STEP : S])

@@ -42,8 +42,8 @@ def tile_list_tabhs_gelu_kernel(tc, tab, w, b, wgo, offs, offs2, out):
         w1 = w[:, P:M].rearrange("(p j) n -> p j n", j=4)
         nc.sync.dma_start(rows[LIVE:P, :].bitcast(I32), scale_rows.bitcast(I32))
         nc.sync.dma_start(idx[:], offs)
-        nc.sync.dma_start(carried[:], w1[P // 2 : P, 2:4, :])
-        nc.sync.dma_start(w_raw1[0 : P // 2, 2:4, :], w1[0 : P // 2, 2:4, :])
+        nc.scalar.dma_start(carried[:], w1[P // 2 : P, 2:4, :])
+        nc.scalar.dma_start(w_raw1[0 : P // 2, 2:4, :], w1[0 : P // 2, 2:4, :])
         nc.sync.dma_start(w_raw1[:, 0:2, :], w1[:, 0:2, :])
         nc.sync.dma_start(words[:], tab[0, 0 : 512 * T].rearrange("(p c) -> p c", p=P).bitcast(I32))
         nc.sync.dma_start(idx2[:], offs2)

@@ -45,19 +45,18 @@ def tile_list_tabhs_gelu_kernel(tc, tab, w, b, wgo, offs, offs2, out):
         nc.scalar.dma_start(carried[:], w1[P // 2 : P, 2:4, :])
         nc.scalar.dma_start(w_raw1[0 : P // 2, 2:4, :], w1[0 : P // 2, 2:4, :])
         nc.sync.dma_start(w_raw1[:, 0:2, :], w1[:, 0:2, :])
-        nc.sync.dma_start(words[:], tab[0, 0 : 512 * T].rearrange("(p c) -> p c", p=P).bitcast(I32))
         nc.sync.dma_start(idx2[:], offs2)
+        nc.sync.dma_start(words[:], tab[0, 0 : 512 * T].rearrange("(p c) -> p c", p=P).bitcast(I32))
 
         def clear(ap, n, value):
             nc.vector.memset(ap[:, 0 : n // 2 - 1], value)
             nc.vector.memset(ap[:, n // 2 - 1 : n], value)
 
         nc.gpsimd.memset(rows[0:LIVE, :].bitcast(I32), 0)
-        warm = keep.tile([P, 16], F32, name="warm")
-        nc.gpsimd.memset(warm[:, 0:1], 0.0)
-        nc.scalar.activation(warm[:, 8:9], warm[:, 0:1], GELU)
         clear(window1[:], SHARE, 0.0)
         nc.gpsimd.memset(window1[:, SHARE:T], 0.0)
+        zero = keep.tile([P, 1], F32, name="zero")
+        nc.gpsimd.memset(zero[:], 0.0)
 
         group = [keep.tile([P, P, 4], BF16, name="group0", align_bytes=256), group1]
         w_scales = [keep.tile([P, P], U8, name="w_scales%d" % m, align_bytes=256) for m in range(2)]
@@ -77,8 +76,10 @@ def tile_list_tabhs_gelu_kernel(tc, tab, w, b, wgo, offs, offs2, out):
         nc.vector.tensor_copy(picked_early[:], rows[:].indirect(idx[:, 0 : EARLY // 16]))
         nc.scalar.copy(w_raw1[P // 2 : P, 2:4, :].rearrange("p j n -> p (j n)"), carried[:].rearrange("p j n -> p (j n)"))
         cast(group1[:], w_raw1[:])
+        warm = turns.tile([P, 1], F32, name="warm", align_bytes=256, offset=2304)
+        nc.scalar.activation(warm[:], zero[:], GELU)
         plane = keep.tile([P, S], U8, name="plane", align_bytes=256)
-        picked_late = turns.tile([P, S - EARLY], U8, name="picked_late", align_bytes=256, offset=2304)
+        picked_late = turns.tile([P, S - EARLY], U8, name="picked_late", align_bytes=256, offset=2560)
 
         def move_scales(picked, lo, hi):
             for r in range(4):

@@ -32,7 +32,6 @@ def tile_list_tabhs_gelu_kernel(tc, tab, w, b, wgo, offs, offs2, out):
         idx = keep.tile([P, S // 16], U16, name="idx", align_bytes=256)
         idx2 = keep.tile([P, S // 16], U16, name="idx2", align_bytes=256)
         words = keep.tile([P, T], I32, name="words", align_bytes=256)
-        carried = keep.tile([P // 2, 2, P], F32, name="carried", align_bytes=256)
         window1 = keep.tile([P, T], F32, name="window1", align_bytes=256)
         w_raw1 = turns.tile([P, 4, P], F32, name="w_raw1", align_bytes=256, offset=1024)
         group1 = turns.tile([P, P, 4], BF16, name="group1", align_bytes=256, offset=5376)
@@ -42,9 +41,7 @@ def tile_list_tabhs_gelu_kernel(tc, tab, w, b, wgo, offs, offs2, out):
         w1 = w[:, P:M].rearrange("(p j) n -> p j n", j=4)
         nc.sync.dma_start(rows[LIVE:P, :].bitcast(I32), scale_rows.bitcast(I32))
         nc.sync.dma_start(idx[:], offs)
-        nc.scalar.dma_start(carried[:], w1[P // 2 : P, 2:4, :])
-        nc.scalar.dma_start(w_raw1[0 : P // 2, 2:4, :], w1[0 : P // 2, 2:4, :])
-        nc.sync.dma_start(w_raw1[:, 0:2, :], w1[:, 0:2, :])
+        nc.sync.dma_start(w_raw1[:], w1)
         nc.sync.dma_start(idx2[:], offs2)
         nc.sync.dma_start(words[:], tab[0, 0 : 512 * T].rearrange("(p c) -> p c", p=P).bitcast(I32))
 
@@ -74,7 +71,6 @@ def tile_list_tabhs_gelu_kernel(tc, tab, w, b, wgo, offs, offs2, out):
 
         picked_early = keep.tile([P, EARLY], U8, name="picked_early", align_bytes=256)
         nc.vector.tensor_copy(picked_early[:], rows[:].indirect(idx[:, 0 : EARLY // 16]))
-        nc.scalar.copy(w_raw1[P // 2 : P, 2:4, :].rearrange("p j n -> p (j n)"), carried[:].rearrange("p j n -> p (j n)"))
         cast(group1[:], w_raw1[:])
         warm = turns.tile([P, 1], F32, name="warm", align_bytes=256, offset=2304)
         nc.scalar.activation(warm[:], zero[:], GELU)
@@ -103,8 +99,8 @@ def tile_list_tabhs_gelu_kernel(tc, tab, w, b, wgo, offs, offs2, out):
             nc.sync.dma_start(bias0[:], b[0:P].rearrange("(p c) -> p c", c=1))
         move_scales(picked_late, EARLY, S)
         factor1 = turns.tile([P, S - STEP], F32, name="factor1", align_bytes=256, offset=22784)
-        nc.sync.dma_start(factor1[:, 0 : 3 * STEP], wgo[:, STEP : 4 * STEP])
-        nc.sync.dma_start(factor1[:, 3 * STEP :], wgo[:, 4 * STEP : S])
+        for lo, hi in ((1, 3), (3, 4), (4, 5), (5, 8)):
+            nc.sync.dma_start(factor1[:, (lo - 1) * STEP : (hi - 1) * STEP], wgo[:, lo * STEP : hi * STEP])
         bias = [bias0, bias1]
 
         def gather_words(dst, lo, hi):

@@ -19,7 +19,7 @@ BANK = 512
 STEP = 256
 LIVE = 112
 SHARE = 2048
-EARLY = 576
+EARLY = 640
 
 
 def tile_list_tabhs_gelu_kernel(tc, tab, w, b, wgo, offs, offs2, out):

import concourse.mybir as mybir

K, M, T, S = 512, 256, 4096, 2048
P = 128
FLOPS = 2 * K * M * S

F32 = mybir.dt.float32
BF16 = mybir.dt.bfloat16
I32 = mybir.dt.int32
U32 = mybir.dt.uint32
U16 = mybir.dt.uint16
U8 = mybir.dt.uint8
FP8X4 = mybir.dt.float8_e4m3fn_x4
COPY = mybir.ActivationFunctionType.Copy
GELU = mybir.ActivationFunctionType.Gelu_apprx_tanh
MULT = mybir.AluOpType.mult

BANK = 512
STEP = 256
LIVE = 112
SHARE = 2048
EARLY = 640


def tile_list_tabhs_gelu_kernel(tc, tab, w, b, wgo, offs, offs2, out):
    nc = tc.nc
    with (
        tc.tile_pool(name="keep", bufs=1) as keep,
        tc.tile_pool(name="turns", bufs=1) as turns,
        tc.psum_pool(name="psum", bufs=1) as psum,
    ):
        idx = keep.tile([P, S // 16], U16, name="idx", align_bytes=256)
        idx2 = keep.tile([P, S // 16], U16, name="idx2", align_bytes=256)
        words = keep.tile([P, T], I32, name="words", align_bytes=256)
        window1 = keep.tile([P, T], F32, name="window1", align_bytes=256)
        w_raw1 = turns.tile([P, 4, P], F32, name="w_raw1", align_bytes=256, offset=1024)
        group1 = turns.tile([P, P, 4], BF16, name="group1", align_bytes=256, offset=5376)
        rows = turns.tile([P, T], U8, name="rows", align_bytes=256, offset=22528)

        scale_rows = tab[0, 512 * T : 528 * T].rearrange("(q t) -> q t", t=T)
        w1 = w[:, P:M].rearrange("(p j) n -> p j n", j=4)
        nc.sync.dma_start(rows[LIVE:P, :].bitcast(I32), scale_rows.bitcast(I32))
        nc.sync.dma_start(idx[:], offs)
        nc.sync.dma_start(w_raw1[:], w1)
        nc.sync.dma_start(idx2[:], offs2)
        nc.sync.dma_start(words[:], tab[0, 0 : 512 * T].rearrange("(p c) -> p c", p=P).bitcast(I32))

        def clear(ap, n, value):
            nc.vector.memset(ap[:, 0 : n // 2 - 1], value)
            nc.vector.memset(ap[:, n // 2 - 1 : n], value)

        nc.gpsimd.memset(rows[0:LIVE, :].bitcast(I32), 0)
        clear(window1[:], SHARE, 0.0)
        nc.gpsimd.memset(window1[:, SHARE:T], 0.0)
        zero = keep.tile([P, 1], F32, name="zero")
        nc.gpsimd.memset(zero[:], 0.0)

        group = [keep.tile([P, P, 4], BF16, name="group0", align_bytes=256), group1]
        w_scales = [keep.tile([P, P], U8, name="w_scales%d" % m, align_bytes=256) for m in range(2)]
        w_codes = [keep.tile([P, P], U32, name="w_codes%d" % m, align_bytes=256) for m in range(2)]

        def cast(dst, src):
            nc.scalar.activation(dst.rearrange("p (c i) j -> p c j i", i=4), src.rearrange("p j (c i) -> p c j i", i=4), COPY)

        def quantise(m):
            nc.vector.quantize_mx(
                out=w_codes[m][:].bitcast(FP8X4),
                scales=w_scales[m][:],
                in_=group[m][:].rearrange("p n j -> p (n j)"),
            )

        picked_early = keep.tile([P, EARLY], U8, name="picked_early", align_bytes=256)
        nc.vector.tensor_copy(picked_early[:], rows[:].indirect(idx[:, 0 : EARLY // 16]))
        cast(group1[:], w_raw1[:])
        warm = turns.tile([P, 1], F32, name="warm", align_bytes=256, offset=2304)
        nc.scalar.activation(warm[:], zero[:], GELU)
        plane = keep.tile([P, S], U8, name="plane", align_bytes=256)
        picked_late = turns.tile([P, S - EARLY], U8, name="picked_late", align_bytes=256, offset=2560)

        def move_scales(picked, lo, hi):
            for r in range(4):
                nc.sync.dma_start(plane[r:P:32, lo:hi].bitcast(I32), picked[LIVE + r : P : 4, :].bitcast(I32))

        move_scales(picked_early, 0, EARLY)
        w_raw0 = turns.tile([P, 4, P], F32, name="w_raw0", align_bytes=256, offset=0)
        nc.sync.dma_start(w_raw0[:], w[:, 0:P].rearrange("(p j) n -> p j n", j=4))
        bias1 = turns.tile([P, 1], F32, name="bias1", align_bytes=256, offset=2048)
        with nc.allow_non_contiguous_dma(reason="128 values, one to a partition"):
            nc.sync.dma_start(bias1[:], b[P:M].rearrange("(p c) -> p c", c=1))
        quantise(1)
        factor0 = turns.tile([P, STEP], F32, name="factor0", align_bytes=256, offset=4608)
        nc.sync.dma_start(factor0[:], wgo[:, 0:STEP])
        window0 = turns.tile([P, T], F32, name="window0", align_bytes=256, offset=6144)
        nc.gpsimd.memset(window0[:], 0.0)
        nc.vector.tensor_copy(picked_late[:], rows[:].indirect(idx[:, EARLY // 16 : S // 16]))

        bias0 = turns.tile([P, 1], F32, name="bias0", align_bytes=256, offset=22528)
        with nc.allow_non_contiguous_dma(reason="128 values, one to a partition"):
            nc.sync.dma_start(bias0[:], b[0:P].rearrange("(p c) -> p c", c=1))
        move_scales(picked_late, EARLY, S)
        factor1 = turns.tile([P, S - STEP], F32, name="factor1", align_bytes=256, offset=22784)
        for lo, hi in ((1, 3), (3, 4), (4, 5), (5, 8)):
            nc.sync.dma_start(factor1[:, (lo - 1) * STEP : (hi - 1) * STEP], wgo[:, lo * STEP : hi * STEP])
        bias = [bias0, bias1]

        def gather_words(dst, lo, hi):
            nc.vector.tensor_copy(dst, words[:].bitcast(U32).indirect(idx[:, lo // 16 : hi // 16]))

        first = keep.tile([P, STEP], U32, name="first", align_bytes=256)
        cover = keep.tile([P, BANK], U32, name="cover", align_bytes=256)
        gather_words(first[:], 0, STEP)
        gather_words(cover[:], STEP, 3 * STEP)
        cast(group[0][:], w_raw0[:])
        quantise(0)

        windows = [window0, window1]
        y = [keep.tile([P, S], F32, name="y%d" % m, align_bytes=256) for m in range(2)]

        slots = [first[:], cover[:, 0:STEP], cover[:, STEP:BANK]]

        def project(tag, *jobs):
            bank = psum.tile([P, BANK], F32, tag=tag, name="bank%d_%d" % jobs[0][0:2])
            spans, at = [], 0
            for m, lo, hi in jobs:
                spans.append((at, at + hi - lo))
                for start in range(lo, hi, STEP):
                    n = min(STEP, hi - start)
                    nc.tensor.matmul_mx(
                        out=bank[:, at : at + n],
                        lhsT=w_codes[m][:].bitcast(FP8X4),
                        lhsT_scale=w_scales[m][:],
                        rhs=slots[start // STEP % 3][:, start % STEP : start % STEP + n].bitcast(FP8X4),
                        rhs_scale=plane[:, start : start + n],
                        start=True,
                        stop=True,
                    )
                    at = at + n
            for (m, lo, hi), (start, end) in reversed(list(zip(jobs, spans))):
                nc.scalar.activation(y[m][:, lo:hi], bank[:, start:end], GELU, bias=bias[m][:])

        def place(m, lo, hi):
            factor = factor0[:] if hi == STEP else factor1[:, lo - STEP : hi - STEP]
            nc.vector.tensor_tensor(windows[m][:].indirect(idx2[:, lo // 16 : hi // 16]), y[m][:, lo:hi], factor, MULT)

        def gather_block(block):
            gather_words(slots[block % 3], block * STEP, (block + 1) * STEP)

        project("a", (1, 0, P))
        project("b", (1, P, STEP))
        place(1, 0, STEP)
        project("a", (1, STEP, 2 * STEP))
        project("b", (0, 0, STEP))
        gather_block(3)
        place(0, 0, STEP)
        project("b", (0, STEP, 2 * STEP), (1, 2 * STEP, 3 * STEP))
        gather_block(4)
        place(1, STEP, 3 * STEP)
        project("b", (0, 2 * STEP, 4 * STEP))
        gather_block(5)
        place(0, STEP, 4 * STEP)
        project("b", (1, 3 * STEP, 5 * STEP))
        gather_block(6)
        place(1, 3 * STEP, 5 * STEP)
        project("b", (0, 4 * STEP, 6 * STEP))
        gather_block(7)
        place(0, 4 * STEP, 5 * STEP)
        project("b", (1, 5 * STEP, 7 * STEP))
        project("b", (1, 7 * STEP, S))
        place(1, 5 * STEP, S)
        project("b", (0, 6 * STEP, S))
        place(0, 5 * STEP, S)
        for m in (1, 0):
            nc.sync.dma_start(out[P * m : P * m + P, :], windows[m][:])
